import numpy as np
import ml_dtypes


def mxq(x, axis, fmt="e4m3"):
    dtype, down = {"e4m3": (ml_dtypes.float8_e4m3fn, 7), "e5m2": (ml_dtypes.float8_e5m2, 14)}[fmt]
    v = np.moveaxis(np.asarray(x, np.float32).astype(ml_dtypes.bfloat16).astype(np.float64), axis, -1)
    blocks = v.reshape(v.shape[:-1] + (-1, 32))
    amax = np.abs(blocks).max(-1, keepdims=True)
    byte = np.maximum(np.where(amax > 0, np.frexp(amax)[1] - 1 + 127, 0) - down, 1)
    scale = np.exp2(byte - 127.0)
    codes = (blocks / scale).astype(np.float32).astype(dtype).astype(np.float64)
    return np.moveaxis((codes * scale).reshape(v.shape), -1, axis)


WIDE = False


def mx_kscale(k):
    if not WIDE:
        return np.ones(k)
    levels = np.array([10, -10, 5, -5, 0])
    if k % 512:
        return np.exp2(np.random.permutation(np.resize(levels, k // 32))).repeat(32)
    a = np.empty((k // 512, 16))
    for p in range(k // 512):
        a[p, :8] = np.random.permutation(np.resize(levels, 8))
        for g in range(8):
            far = levels[np.abs(levels - a[p, g]) >= 10]
            a[p, g + 8] = far[np.random.randint(len(far))]
    return np.exp2(a.ravel()).repeat(32)


def f64(x):
    return np.asarray(x).astype(np.float64)


def striped(idx):
    return np.tile(idx.reshape(-1, 16).T, (8, 1)).astype(np.uint16)


def unstriped(offs):
    return offs[:16].T.reshape(-1).astype(np.int64)


E2M1 = np.array([0.0, 0.5, 1.0, 1.5, 2.0, 3.0, 4.0, 6.0, -0.0, -0.5, -1.0, -1.5, -2.0, -3.0, -4.0, -6.0])


def pack_weight(w, fmt):
    k, n = w.shape
    w = f64(np.asarray(w, np.float32).astype(ml_dtypes.bfloat16)).reshape(k // 32, 32, n)
    amax = np.abs(w).max(1)
    if fmt == "e4m3":
        byte = np.frexp(amax)[1] - 1 + 127 - 7
    else:
        mant, ex = np.frexp(amax / 6.0)
        byte = np.where(mant > 0.5, ex, ex - 1) + 127
    byte = np.clip(np.where(amax > 0, byte, 1), 1, 254)
    scaled = (w * np.exp2(127.0 - byte)[:, None, :]).reshape(k, n).astype(np.float32)
    by_word = np.ascontiguousarray(scaled.reshape(k // 512, 128, 4, n).transpose(0, 1, 3, 2))
    if fmt == "e4m3":
        words = by_word.astype(ml_dtypes.float8_e4m3fn).view(np.uint8)
    else:
        c = by_word.astype(ml_dtypes.float4_e2m1fn).view(np.uint8) & 0xF
        words = (c[..., 0::2] | (c[..., 1::2] << 4)).reshape(k // 512, 128, 2 * n)
    return np.ascontiguousarray(words), np.ascontiguousarray(byte.astype(np.uint8).reshape(k // 512, 16, n))


def unpack_weight(words, scales, fmt):
    g, _, n = scales.shape
    words = np.ascontiguousarray(words).reshape(g, 128, n, -1)
    if fmt == "e4m3":
        vals = words.view(ml_dtypes.float8_e4m3fn).astype(np.float64)
    else:
        nib = np.empty((g, 128, n, 4), np.uint8)
        nib[..., 0::2] = words & 0xF
        nib[..., 1::2] = words >> 4
        vals = E2M1[nib]
    vals = vals * np.repeat(np.exp2(scales.astype(np.float64) - 127.0), 8, axis=1)[..., None]
    return vals.transpose(0, 1, 3, 2).reshape(g * 512, n)


def silu(v):
    return v / (1.0 + np.exp(-np.maximum(v, -700.0)))


K, M, T, S = 1536, 256, 2048, 1024


def setup_inputs():
    n = np.random.standard_normal
    s = mx_kscale(K)[:, None]
    v = pack_weight(n((K, T)) * s, "e4m3")
    return {
        "tab_words": v[0],
        "tab_scales": v[1],
        "w": (n((K, M)) / np.sqrt(K) / s).astype(np.float32),
        "ts": np.tile(np.exp(0.5 * n(T)), (128, 1)).astype(np.float32),
        "b": (0.3 * n(256)).astype(np.float32),
        "offs": striped(np.random.permutation(T)[:S]),
    }


def reference(tab_words, tab_scales, w, ts, b, offs):
    tab_ = unpack_weight(tab_words, tab_scales, "e4m3")[:, unstriped(offs)]
    w_ = mxq(f64(w), 0, "e4m3")
    y = w_.T @ tab_
    y = y * f64(ts)[0][unstriped(offs)]
    return silu(y + f64(b)[:, None])

@@ -1,0 +1,194 @@
+from contextlib import ExitStack
+
+import concourse.mybir as mybir
+from concourse.masks import make_identity
+
+K, M, T, S = 1536, 256, 2048, 1024
+FLOPS = 2 * K * M * S
+BYTES = K * T + (K // 32) * T + 4 * K * M + 4 * T + 4 * M + 2 * 128 * (S // 16) + 4 * M * S
+
+F32 = mybir.dt.float32
+BF16 = mybir.dt.bfloat16
+I32 = mybir.dt.int32
+U32 = mybir.dt.uint32
+U16 = mybir.dt.uint16
+U8 = mybir.dt.uint8
+FP8X4 = mybir.dt.float8_e4m3fn_x4
+ACT = mybir.ActivationFunctionType
+MULT = mybir.AluOpType.mult
+
+P = 128
+PASSES = K // 512
+SLICE = 256
+N_SLICES = S // SLICE
+N_TURNED = 2
+TS_ROW = P - 1
+
+
+def tile_list_tabts_silu_kernel(tc, tab_words, tab_scales, w, ts, b, offs, out):
+    nc = tc.nc
+    with ExitStack() as ctx:
+        keep = ctx.enter_context(tc.tile_pool(name="keep", bufs=1))
+        psum = ctx.enter_context(tc.psum_pool(name="psum", bufs=1))
+
+        offsets = keep.tile([P, S // 16], U16, name="offsets")
+        ts_window = keep.tile([P, T], F32, name="ts_window")
+        scale_window = keep.tile([P, T // 4], I32, name="scale_window")
+        word_window = [keep.tile([P, T], I32, name=f"word_window{a}") for a in range(PASSES)]
+        w_raw = [keep.tile([P, 4, M], F32, name=f"w_raw{a}") for a in range(PASSES)]
+        w_bf16 = [keep.tile([P, M, 4], BF16, name=f"w_bf16_{a}", align_bytes=64) for a in range(PASSES)]
+        w_codes = [keep.tile([P, M], U32, name=f"w_codes{a}", align_bytes=64) for a in range(PASSES)]
+        w_scales = [keep.tile([P, M], U8, name=f"w_scales{a}", align_bytes=64) for a in range(PASSES)]
+        v_codes = [keep.tile([P, S], U32, name=f"v_codes{a}", align_bytes=64) for a in range(PASSES)]
+        v_scales = keep.tile([P, S], U8, name="v_scales", align_bytes=64)
+        ts_picked = keep.tile([P, S], F32, name="ts_picked")
+        ts_cols = keep.tile([P, S // P], F32, name="ts_cols")
+        bias = keep.tile([P, 2], F32, name="bias")
+        ident = keep.tile([P, P], F32, name="ident")
+        warm_in = keep.tile([P, 1], F32, name="warm_in")
+        warm_out = keep.tile([P, 1], F32, name="warm_out")
+        banks = [psum.tile([P, 512], F32, name=f"bank{i}") for i in range(8)]
+
+        nc.sync.dma_start(offsets[:], offs)
+        nc.sync.dma_start(out=ts_window[TS_ROW:P, :], in_=ts[0:1, :])
+        nc.vector.memset(warm_in[:], 0.0)
+        nc.vector.memset(scale_window[:], 0)
+        nc.vector.memset(ts_window[0:TS_ROW, :], 0.0)
+        nc.scalar.activation(out=warm_out[:], in_=warm_in[:], func=ACT.Silu)
+        make_identity(nc, ident[:])
+
+        def load_words(a):
+            nc.sync.dma_start(out=word_window[a][:], in_=tab_words[a].rearrange("p t i -> p (t i)").bitcast(I32))
+
+        def load_w(a):
+            nc.sync.dma_start(out=w_raw[a][:], in_=w[512 * a : 512 * (a + 1), :].rearrange("(p i) n -> p i n", i=4))
+
+        load_words(0)
+        load_words(1)
+        for a in range(PASSES):
+            load_w(a)
+        load_words(2)
+        for q in range(4):
+            nc.gpsimd.dma_start(
+                out=scale_window[32 * q : 32 * q + 4 * PASSES, :],
+                in_=tab_scales[:, 4 * q : 4 * q + 4, :].bitcast(I32),
+            )
+        with nc.allow_non_contiguous_dma(reason="one bias value a partition"):
+            nc.scalar.dma_start(out=bias[:], in_=b.rearrange("(h p) -> p h", p=P))
+
+        def listed(lo, hi):
+            return offsets[:, lo // 16 : hi // 16]
+
+        def gather_words(a, lo, hi):
+            nc.vector.tensor_copy(out=v_codes[a][:, lo:hi], in_=word_window[a][:].bitcast(U32).indirect(listed(lo, hi)))
+
+        def gather_scales(lo, hi):
+            nc.vector.tensor_copy(out=v_scales[:, lo:hi], in_=scale_window[:].bitcast(U8).indirect(listed(lo, hi)))
+
+        def cast_w(a):
+            nc.scalar.copy(out=w_bf16[a][:], in_=w_raw[a][:].rearrange("p i n -> p n i"))
+
+        def quantize_w(a):
+            nc.vector.quantize_mx(
+                out=w_codes[a][:].bitcast(FP8X4),
+                scales=w_scales[a][:],
+                in_=w_bf16[a][:].rearrange("p n i -> p (n i)"),
+            )
+
+        nc.vector.tensor_copy(out=ts_picked[:], in_=ts_window[:].indirect(listed(0, S)))
+        for half in range(2):
+            for u in range(4):
+                j0 = (4 * half + u) * P
+                nc.tensor.transpose(banks[half][:, u * P : (u + 1) * P], ts_picked[:, j0 : j0 + P], ident[:])
+            nc.scalar.copy(
+                out=ts_cols[:, 4 * half : 4 * half + 4],
+                in_=banks[half][:].rearrange("p (u c) -> p u c", c=P)[:, :, TS_ROW],
+            )
+        first_straight = N_TURNED * SLICE
+        n_straight = S - first_straight
+        ts_rows = keep.tile([P, max(n_straight, 1)], F32, name="ts_rows")
+        for c0 in range(0, n_straight, 512):
+            width = min(512, n_straight - c0)
+            bank = banks[2 + c0 // 512]
+            for u in range(width // P):
+                t = (first_straight + c0) // P + u
+                nc.tensor.transpose(bank[:, u * P : (u + 1) * P], ts_cols[:, t : t + 1].to_broadcast([P, P]), ident[:])
+            nc.scalar.copy(out=ts_rows[:, c0 : c0 + width], in_=bank[:, 0:width])
+
+        def matmuls(s, a):
+            flags = dict(start=(a == 0), stop=(a == PASSES - 1))
+            for h in range(2):
+                acc = banks[2 * s + h][:, 0:256]
+                if s < N_TURNED:
+                    cols = slice(s * SLICE + h * P, s * SLICE + (h + 1) * P)
+                    nc.tensor.matmul_mx(
+                        out=acc,
+                        lhsT=v_codes[a][:, cols].bitcast(FP8X4), lhsT_scale=v_scales[4 * a : P, cols],
+                        rhs=w_codes[a][:].bitcast(FP8X4), rhs_scale=w_scales[a][:],
+                        **flags,
+                    )
+                else:
+                    cols = slice(s * SLICE, (s + 1) * SLICE)
+                    chans = slice(h * P, (h + 1) * P)
+                    nc.tensor.matmul_mx(
+                        out=acc,
+                        lhsT=w_codes[a][:, chans].bitcast(FP8X4), lhsT_scale=w_scales[a][:, chans],
+                        rhs=v_codes[a][:, cols].bitcast(FP8X4), rhs_scale=v_scales[4 * a : P, cols],
+                        **flags,
+                    )
+
+        scaled = [[keep.tile([P, SLICE], F32, name=f"scaled{s}_{h}") for h in range(2)] for s in range(N_SLICES)]
+        result = [[keep.tile([P, SLICE], F32, name=f"result{s}_{h}") for h in range(2)] for s in range(N_SLICES)]
+
+        def scale(s):
+            for h in range(2):
+                acc = banks[2 * s + h][:, 0:256]
+                if s < N_TURNED:
+                    t = 2 * s + h
+                    nc.scalar.activation(out=scaled[s][h][:], in_=acc, func=ACT.Copy, scale=ts_cols[:, t : t + 1])
+                else:
+                    c0 = s * SLICE - first_straight
+                    nc.vector.tensor_tensor(out=scaled[s][h][:], in0=acc, in1=ts_rows[:, c0 : c0 + SLICE], op=MULT)
+
+        def turn_back(s):
+            for h in range(2):
+                for u in range(2):
+                    nc.tensor.transpose(
+                        banks[2 * s + h][:, 256 + u * P : 256 + (u + 1) * P],
+                        scaled[s][u][:, h * P : (h + 1) * P],
+                        ident[:],
+                    )
+
+        def finish(s):
+            for h in range(2):
+                pre = banks[2 * s + h][:, 256:512] if s < N_TURNED else scaled[s][h][:]
+                nc.scalar.activation(out=result[s][h][:], in_=pre, func=ACT.Silu, bias=bias[:, h : h + 1])
+                nc.sync.dma_start(out=out[h * P : (h + 1) * P, s * SLICE : (s + 1) * SLICE], in_=result[s][h][:])
+
+        gather_words(0, 0, S)
+        gather_words(1, 0, S)
+        for a in range(PASSES):
+            cast_w(a)
+        gather_scales(0, 512)
+        for a in range(PASSES):
+            quantize_w(a)
+        for a in range(2):
+            for s in range(2):
+                matmuls(s, a)
+        for s in range(2):
+            gather_words(2, s * SLICE, (s + 1) * SLICE)
+            matmuls(s, 2)
+            scale(s)
+            turn_back(s)
+        gather_scales(512, S)
+        for a in range(2):
+            for s in range(2, 4):
+                matmuls(s, a)
+        finish(0)
+        finish(1)
+        for s in range(2, 4):
+            gather_words(2, s * SLICE, (s + 1) * SLICE)
+            matmuls(s, 2)
+        for s in range(2, 4):
+            scale(s)
+            finish(s)

@@ -20,8 +20,7 @@ MULT = mybir.AluOpType.mult
 P = 128
 PASSES = K // 512
 SLICE = 256
-N_SLICES = S // SLICE
-N_TURNED = 2
+HALF = S // 2
 TS_ROW = P - 1
 
 
@@ -31,123 +30,123 @@ def tile_list_tabts_silu_kernel(tc, tab_words, tab_scales, w, ts, b, offs, out):
         keep = ctx.enter_context(tc.tile_pool(name="keep", bufs=1))
         psum = ctx.enter_context(tc.psum_pool(name="psum", bufs=1))
 
+        def sbuf(name, shape, dtype, buffer=None):
+            return keep.tile(shape, dtype, name=name, tag=buffer or name, align_bytes=64)
+
         offsets = keep.tile([P, S // 16], U16, name="offsets")
-        ts_window = keep.tile([P, T], F32, name="ts_window")
-        scale_window = keep.tile([P, T // 4], I32, name="scale_window")
-        word_window = [keep.tile([P, T], I32, name=f"word_window{a}") for a in range(PASSES)]
-        w_raw = [keep.tile([P, 4, M], F32, name=f"w_raw{a}") for a in range(PASSES)]
-        w_bf16 = [keep.tile([P, M, 4], BF16, name=f"w_bf16_{a}", align_bytes=64) for a in range(PASSES)]
-        w_codes = [keep.tile([P, M], U32, name=f"w_codes{a}", align_bytes=64) for a in range(PASSES)]
-        w_scales = [keep.tile([P, M], U8, name=f"w_scales{a}", align_bytes=64) for a in range(PASSES)]
-        v_codes = [keep.tile([P, S], U32, name=f"v_codes{a}", align_bytes=64) for a in range(PASSES)]
-        v_scales = keep.tile([P, S], U8, name="v_scales", align_bytes=64)
-        ts_picked = keep.tile([P, S], F32, name="ts_picked")
-        ts_cols = keep.tile([P, S // P], F32, name="ts_cols")
-        bias = keep.tile([P, 2], F32, name="bias")
-        ident = keep.tile([P, P], F32, name="ident")
-        warm_in = keep.tile([P, 1], F32, name="warm_in")
-        warm_out = keep.tile([P, 1], F32, name="warm_out")
+        ts_window = sbuf("ts_window", [P, T], F32)
+        scale_window = sbuf("scale_window", [P, T // 4], I32)
+        w_raw = sbuf("w_raw", [P, PASSES, 4, M], F32)
+        w_bf16 = [sbuf(f"w_bf16_{a}", [P, M, 4], BF16) for a in range(PASSES)]
+        ts_picked = sbuf("ts_picked", [P, S], F32)
+        ts_cols = [sbuf(f"ts_cols{half}", [P, 4], F32) for half in range(2)]
+        ts_rows = sbuf("ts_rows", [P, HALF], F32)
+        bias = sbuf("bias", [P, 2], F32)
+        ident = sbuf("ident", [P, P], F32)
+        warm = sbuf("warm", [P, 1], F32)
         banks = [psum.tile([P, 512], F32, name=f"bank{i}") for i in range(8)]
-
-        nc.sync.dma_start(offsets[:], offs)
-        nc.sync.dma_start(out=ts_window[TS_ROW:P, :], in_=ts[0:1, :])
-        nc.vector.memset(warm_in[:], 0.0)
-        nc.vector.memset(scale_window[:], 0)
-        nc.vector.memset(ts_window[0:TS_ROW, :], 0.0)
-        nc.scalar.activation(out=warm_out[:], in_=warm_in[:], func=ACT.Silu)
-        make_identity(nc, ident[:])
-
-        def load_words(a):
-            nc.sync.dma_start(out=word_window[a][:], in_=tab_words[a].rearrange("p t i -> p (t i)").bitcast(I32))
-
-        def load_w(a):
-            nc.sync.dma_start(out=w_raw[a][:], in_=w[512 * a : 512 * (a + 1), :].rearrange("(p i) n -> p i n", i=4))
-
-        load_words(0)
-        load_words(1)
-        for a in range(PASSES):
-            load_w(a)
-        load_words(2)
-        for q in range(4):
-            nc.gpsimd.dma_start(
-                out=scale_window[32 * q : 32 * q + 4 * PASSES, :],
-                in_=tab_scales[:, 4 * q : 4 * q + 4, :].bitcast(I32),
-            )
-        with nc.allow_non_contiguous_dma(reason="one bias value a partition"):
-            nc.scalar.dma_start(out=bias[:], in_=b.rearrange("(h p) -> p h", p=P))
 
         def listed(lo, hi):
             return offsets[:, lo // 16 : hi // 16]
 
-        def gather_words(a, lo, hi):
-            nc.vector.tensor_copy(out=v_codes[a][:, lo:hi], in_=word_window[a][:].bitcast(U32).indirect(listed(lo, hi)))
+        def load_words(a, buffer=None):
+            window = sbuf(f"word_window{a}", [P, T], I32, buffer)
+            nc.sync.dma_start(out=window[:], in_=tab_words[a].rearrange("p t i -> p (t i)").bitcast(I32))
+            return window
 
-        def gather_scales(lo, hi):
-            nc.vector.tensor_copy(out=v_scales[:, lo:hi], in_=scale_window[:].bitcast(U8).indirect(listed(lo, hi)))
+        def load_w(a0, a1):
+            nc.sync.dma_start(
+                out=w_raw[:, a0:a1].rearrange("p a i n -> p a (i n)"),
+                in_=w[512 * a0 : 512 * a1, :].rearrange("(a p i) n -> p a (i n)", p=P, i=4),
+            )
 
-        def cast_w(a):
-            nc.scalar.copy(out=w_bf16[a][:], in_=w_raw[a][:].rearrange("p i n -> p n i"))
+        nc.sync.dma_start(offsets[:], offs)
+        nc.sync.dma_start(out=ts_window[TS_ROW:P, :], in_=ts[0:1, :])
+        nc.vector.memset(scale_window[:], 0)
+        nc.vector.memset(ts_window[0:TS_ROW, :], 0.0)
+        make_identity(nc, ident[:])
+        window0 = load_words(0)
+        load_w(0, 2)
+        window1 = load_words(1)
+        load_w(2, 3)
+        for q in range(4):
+            nc.scalar.dma_start(
+                out=scale_window[32 * q : 32 * q + 4 * PASSES, :],
+                in_=tab_scales[:, 4 * q : 4 * q + 4, :].bitcast(I32),
+            )
+        with nc.allow_non_contiguous_dma(reason="one bias value a partition"):
+            nc.gpsimd.dma_start(out=bias[:], in_=b.rearrange("(h p) -> p h", p=P))
 
-        def quantize_w(a):
+        nc.vector.tensor_copy(out=ts_picked[:], in_=ts_window[:].indirect(listed(0, S)))
+        window2 = load_words(2, "ts_window")
+        nc.scalar.activation(out=warm[:], in_=ts_picked[:, 0:1], func=ACT.Silu)
+        for half in (1, 0):
+            for u in range(4):
+                j0 = (4 * half + u) * P
+                nc.tensor.transpose(banks[5 + half][:, u * P : (u + 1) * P], ts_picked[:, j0 : j0 + P], ident[:])
+            nc.scalar.copy(
+                out=ts_cols[half][:],
+                in_=banks[5 + half][:].rearrange("p (u c) -> p u c", c=P)[:, :, TS_ROW],
+            )
+        for u in range(4):
+            nc.tensor.transpose(banks[7][:, u * P : (u + 1) * P], ts_cols[1][:, u : u + 1].to_broadcast([P, P]), ident[:])
+        nc.scalar.copy(out=ts_rows[:], in_=banks[7][:])
+        for a in range(PASSES):
+            nc.scalar.copy(out=w_bf16[a][:], in_=w_raw[:, a].rearrange("p i n -> p n i"))
+
+        v_codes = {}
+
+        def gather_words(a, window, lo, hi, buffer=None, step=None):
+            codes = sbuf(f"v_codes{a}_{lo}", [P, hi - lo], U32, buffer)
+            for s in range(lo // SLICE, hi // SLICE):
+                v_codes[a, s] = codes[:, s * SLICE - lo : (s + 1) * SLICE - lo]
+            for c in range(lo, hi, step or hi - lo):
+                c1 = c + (step or hi - lo)
+                nc.vector.tensor_copy(out=codes[:, c - lo : c1 - lo], in_=window[:].bitcast(U32).indirect(listed(c, c1)))
+
+        w_codes, w_scales = {}, {}
+
+        def quantize_w(a, codes_buffer=None, scales_buffer=None):
+            w_codes[a] = sbuf(f"w_codes{a}", [P, M], U32, codes_buffer)
+            w_scales[a] = sbuf(f"w_scales{a}", [P, M], U8, scales_buffer)
             nc.vector.quantize_mx(
                 out=w_codes[a][:].bitcast(FP8X4),
                 scales=w_scales[a][:],
                 in_=w_bf16[a][:].rearrange("p n i -> p (n i)"),
             )
 
-        nc.vector.tensor_copy(out=ts_picked[:], in_=ts_window[:].indirect(listed(0, S)))
-        for half in range(2):
-            for u in range(4):
-                j0 = (4 * half + u) * P
-                nc.tensor.transpose(banks[half][:, u * P : (u + 1) * P], ts_picked[:, j0 : j0 + P], ident[:])
-            nc.scalar.copy(
-                out=ts_cols[:, 4 * half : 4 * half + 4],
-                in_=banks[half][:].rearrange("p (u c) -> p u c", c=P)[:, :, TS_ROW],
-            )
-        first_straight = N_TURNED * SLICE
-        n_straight = S - first_straight
-        ts_rows = keep.tile([P, max(n_straight, 1)], F32, name="ts_rows")
-        for c0 in range(0, n_straight, 512):
-            width = min(512, n_straight - c0)
-            bank = banks[2 + c0 // 512]
-            for u in range(width // P):
-                t = (first_straight + c0) // P + u
-                nc.tensor.transpose(bank[:, u * P : (u + 1) * P], ts_cols[:, t : t + 1].to_broadcast([P, P]), ident[:])
-            nc.scalar.copy(out=ts_rows[:, c0 : c0 + width], in_=bank[:, 0:width])
-
         def matmuls(s, a):
             flags = dict(start=(a == 0), stop=(a == PASSES - 1))
             for h in range(2):
                 acc = banks[2 * s + h][:, 0:256]
-                if s < N_TURNED:
-                    cols = slice(s * SLICE + h * P, s * SLICE + (h + 1) * P)
+                part = slice(h * P, (h + 1) * P)
+                v_plane = v_scales[4 * a : P, s * SLICE : (s + 1) * SLICE]
+                if s < 2:
                     nc.tensor.matmul_mx(
                         out=acc,
-                        lhsT=v_codes[a][:, cols].bitcast(FP8X4), lhsT_scale=v_scales[4 * a : P, cols],
+                        lhsT=v_codes[a, s][:, part].bitcast(FP8X4), lhsT_scale=v_plane[:, part],
                         rhs=w_codes[a][:].bitcast(FP8X4), rhs_scale=w_scales[a][:],
                         **flags,
                     )
                 else:
-                    cols = slice(s * SLICE, (s + 1) * SLICE)
-                    chans = slice(h * P, (h + 1) * P)
                     nc.tensor.matmul_mx(
                         out=acc,
-                        lhsT=w_codes[a][:, chans].bitcast(FP8X4), lhsT_scale=w_scales[a][:, chans],
-                        rhs=v_codes[a][:, cols].bitcast(FP8X4), rhs_scale=v_scales[4 * a : P, cols],
+                        lhsT=w_codes[a][:, part].bitcast(FP8X4), lhsT_scale=w_scales[a][:, part],
+                        rhs=v_codes[a, s].bitcast(FP8X4), rhs_scale=v_plane,
                         **flags,
                     )
 
-        scaled = [[keep.tile([P, SLICE], F32, name=f"scaled{s}_{h}") for h in range(2)] for s in range(N_SLICES)]
-        result = [[keep.tile([P, SLICE], F32, name=f"result{s}_{h}") for h in range(2)] for s in range(N_SLICES)]
+        scaled = [[sbuf(f"scaled{s}_{h}", [P, SLICE], F32) for h in range(2)] for s in range(4)]
+        result = [[sbuf(f"result{s}_{h}", [P, SLICE], F32) for h in range(2)] for s in range(4)]
 
         def scale(s):
             for h in range(2):
                 acc = banks[2 * s + h][:, 0:256]
-                if s < N_TURNED:
+                if s < 2:
                     t = 2 * s + h
-                    nc.scalar.activation(out=scaled[s][h][:], in_=acc, func=ACT.Copy, scale=ts_cols[:, t : t + 1])
+                    nc.scalar.activation(out=scaled[s][h][:], in_=acc, func=ACT.Copy, scale=ts_cols[0][:, t : t + 1])
                 else:
-                    c0 = s * SLICE - first_straight
+                    c0 = s * SLICE - HALF
                     nc.vector.tensor_tensor(out=scaled[s][h][:], in0=acc, in1=ts_rows[:, c0 : c0 + SLICE], op=MULT)
 
         def turn_back(s):
@@ -161,34 +160,34 @@ def tile_list_tabts_silu_kernel(tc, tab_words, tab_scales, w, ts, b, offs, out):
 
         def finish(s):
             for h in range(2):
-                pre = banks[2 * s + h][:, 256:512] if s < N_TURNED else scaled[s][h][:]
+                pre = banks[2 * s + h][:, 256:512] if s < 2 else scaled[s][h][:]
                 nc.scalar.activation(out=result[s][h][:], in_=pre, func=ACT.Silu, bias=bias[:, h : h + 1])
                 nc.sync.dma_start(out=out[h * P : (h + 1) * P, s * SLICE : (s + 1) * SLICE], in_=result[s][h][:])
 
-        gather_words(0, 0, S)
-        gather_words(1, 0, S)
-        for a in range(PASSES):
-            cast_w(a)
-        gather_scales(0, 512)
-        for a in range(PASSES):
-            quantize_w(a)
-        for a in range(2):
-            for s in range(2):
-                matmuls(s, a)
+        gather_words(0, window0, 0, S)
+        v_scales = sbuf("v_scales", [P, S], U8, "word_window0")
+        nc.vector.tensor_copy(out=v_scales[:], in_=scale_window[:].bitcast(U8).indirect(listed(0, S)))
+        quantize_w(0, "scale_window", "ts_cols1")
+        for s in range(4):
+            matmuls(s, 0)
+        gather_words(1, window1, 0, HALF, "w_bf16_0")
+        quantize_w(1)
         for s in range(2):
-            gather_words(2, s * SLICE, (s + 1) * SLICE)
+            matmuls(s, 1)
+        gather_words(1, window1, HALF, S, "w_bf16_1")
+        quantize_w(2)
+        for s in range(2, 4):
+            matmuls(s, 1)
+        gather_words(2, window2, 0, S, "w_bf16_2", SLICE)
+        for s in range(2):
             matmuls(s, 2)
             scale(s)
-            turn_back(s)
-        gather_scales(512, S)
-        for a in range(2):
-            for s in range(2, 4):
-                matmuls(s, a)
+        turn_back(0)
+        matmuls(2, 2)
+        turn_back(1)
+        matmuls(3, 2)
         finish(0)
         finish(1)
-        for s in range(2, 4):
-            gather_words(2, s * SLICE, (s + 1) * SLICE)
-            matmuls(s, 2)
         for s in range(2, 4):
             scale(s)
             finish(s)

@@ -36,14 +36,14 @@ def tile_list_tabts_silu_kernel(tc, tab_words, tab_scales, w, ts, b, offs, out):
         offsets = keep.tile([P, S // 16], U16, name="offsets")
         ts_window = sbuf("ts_window", [P, T], F32)
         scale_window = sbuf("scale_window", [P, T // 4], I32)
-        w_raw = sbuf("w_raw", [P, PASSES, 4, M], F32)
         w_bf16 = [sbuf(f"w_bf16_{a}", [P, M, 4], BF16) for a in range(PASSES)]
         ts_picked = sbuf("ts_picked", [P, S], F32)
         ts_cols = [sbuf(f"ts_cols{half}", [P, 4], F32) for half in range(2)]
         ts_rows = sbuf("ts_rows", [P, HALF], F32)
         bias = sbuf("bias", [P, 2], F32)
         ident = sbuf("ident", [P, P], F32)
-        warm = sbuf("warm", [P, 1], F32)
+        warm_in = sbuf("warm_in", [P, 1], F32)
+        warm_out = sbuf("warm_out", [P, 1], F32)
         banks = [psum.tile([P, 512], F32, name=f"bank{i}") for i in range(8)]
 
         def listed(lo, hi):
@@ -54,32 +54,34 @@ def tile_list_tabts_silu_kernel(tc, tab_words, tab_scales, w, ts, b, offs, out):
             nc.sync.dma_start(out=window[:], in_=tab_words[a].rearrange("p t i -> p (t i)").bitcast(I32))
             return window
 
-        def load_w(a0, a1):
-            nc.sync.dma_start(
-                out=w_raw[:, a0:a1].rearrange("p a i n -> p a (i n)"),
-                in_=w[512 * a0 : 512 * a1, :].rearrange("(a p i) n -> p a (i n)", p=P, i=4),
-            )
+        def load_w(a, raw):
+            nc.sync.dma_start(out=raw, in_=w[512 * a : 512 * (a + 1), :].rearrange("(p i) n -> p i n", i=4))
 
         nc.sync.dma_start(offsets[:], offs)
         nc.sync.dma_start(out=ts_window[TS_ROW:P, :], in_=ts[0:1, :])
-        nc.vector.memset(scale_window[:], 0)
+        nc.gpsimd.memset(scale_window[:], 0)
+        nc.vector.memset(warm_in[:], 0.0)
         nc.vector.memset(ts_window[0:TS_ROW, :], 0.0)
+        nc.scalar.activation(out=warm_out[:], in_=warm_in[:], func=ACT.Silu)
         make_identity(nc, ident[:])
         window0 = load_words(0)
-        load_w(0, 2)
-        window1 = load_words(1)
-        load_w(2, 3)
+        w_first = sbuf("w_first", [P, 4, M], F32)
+        load_w(0, w_first[:])
+        with nc.allow_non_contiguous_dma(reason="one bias value a partition"):
+            nc.sync.dma_start(out=bias[:], in_=b.rearrange("(h p) -> p h", p=P))
         for q in range(4):
-            nc.scalar.dma_start(
+            nc.sync.dma_start(
                 out=scale_window[32 * q : 32 * q + 4 * PASSES, :],
                 in_=tab_scales[:, 4 * q : 4 * q + 4, :].bitcast(I32),
             )
-        with nc.allow_non_contiguous_dma(reason="one bias value a partition"):
-            nc.gpsimd.dma_start(out=bias[:], in_=b.rearrange("(h p) -> p h", p=P))
+        w_rest = sbuf("w_rest", [P, 2, 4, M], F32, "warm_in")
+        w_raw = [w_first[:], w_rest[:, 0], w_rest[:, 1]]
+        load_w(1, w_raw[1])
+        window1 = load_words(1, "warm_out")
+        load_w(2, w_raw[2])
 
         nc.vector.tensor_copy(out=ts_picked[:], in_=ts_window[:].indirect(listed(0, S)))
         window2 = load_words(2, "ts_window")
-        nc.scalar.activation(out=warm[:], in_=ts_picked[:, 0:1], func=ACT.Silu)
         for half in (1, 0):
             for u in range(4):
                 j0 = (4 * half + u) * P
@@ -92,7 +94,7 @@ def tile_list_tabts_silu_kernel(tc, tab_words, tab_scales, w, ts, b, offs, out):
             nc.tensor.transpose(banks[7][:, u * P : (u + 1) * P], ts_cols[1][:, u : u + 1].to_broadcast([P, P]), ident[:])
         nc.scalar.copy(out=ts_rows[:], in_=banks[7][:])
         for a in range(PASSES):
-            nc.scalar.copy(out=w_bf16[a][:], in_=w_raw[:, a].rearrange("p i n -> p n i"))
+            nc.scalar.copy(out=w_bf16[a][:], in_=w_raw[a].rearrange("p i n -> p n i"))
 
         v_codes = {}
 

@@ -67,8 +67,11 @@ def tile_list_tabts_silu_kernel(tc, tab_words, tab_scales, w, ts, b, offs, out):
         window0 = load_words(0)
         w_first = sbuf("w_first", [P, 4, M], F32)
         load_w(0, w_first[:])
-        with nc.allow_non_contiguous_dma(reason="one bias value a partition"):
-            nc.sync.dma_start(out=bias[:], in_=b.rearrange("(h p) -> p h", p=P))
+        b_rows = sbuf("b_rows", [P, P], F32)
+        nc.gpsimd.memset(b_rows[0 : P - 2, :], 0.0)
+        nc.sync.dma_start(out=b_rows[P - 2 : P, :], in_=b.rearrange("(h p) -> h p", p=P))
+        nc.tensor.transpose(banks[4][:, 0:P], b_rows[:], ident[:])
+        nc.scalar.copy(out=bias[:], in_=banks[4][:, P - 2 : P])
         for q in range(4):
             nc.sync.dma_start(
                 out=scale_window[32 * q : 32 * q + 4 * PASSES, :],

@@ -1,7 +1,6 @@
 from contextlib import ExitStack
 
 import concourse.mybir as mybir
-from concourse.masks import make_identity
 
 K, M, T, S = 1536, 256, 2048, 1024
 FLOPS = 2 * K * M * S
@@ -15,47 +14,47 @@ U16 = mybir.dt.uint16
 U8 = mybir.dt.uint8
 FP8X4 = mybir.dt.float8_e4m3fn_x4
 ACT = mybir.ActivationFunctionType
-MULT = mybir.AluOpType.mult
+ALU = mybir.AluOpType
 
 P = 128
 PASSES = K // 512
-SLICE = 256
-HALF = S // 2
+BANK = 512
 TS_ROW = P - 1
+RAW_BYTES = 4 * M * 4
+WORD_BYTES = 4 * T
+SUMS = [(0, 0, 256), (0, 256, 512), (0, 512, 1024), (1, 0, 512), (1, 512, 768), (1, 768, 1024)]
 
 
 def tile_list_tabts_silu_kernel(tc, tab_words, tab_scales, w, ts, b, offs, out):
     nc = tc.nc
     with ExitStack() as ctx:
         keep = ctx.enter_context(tc.tile_pool(name="keep", bufs=1))
+        late = ctx.enter_context(tc.tile_pool(name="late", bufs=1))
+        first_words = ctx.enter_context(tc.tile_pool(name="first_words", bufs=1))
+        first_weights = ctx.enter_context(tc.tile_pool(name="first_weights", bufs=1))
         psum = ctx.enter_context(tc.psum_pool(name="psum", bufs=1))
 
-        def sbuf(name, shape, dtype, buffer=None):
-            return keep.tile(shape, dtype, name=name, tag=buffer or name, align_bytes=64)
+        def sbuf(name, shape, dtype):
+            return keep.tile(shape, dtype, name=name, align_bytes=64)
+
+        def placed(pool, name, shape, dtype, offset):
+            return pool.tile(shape, dtype, name=name, offset=offset, align_bytes=64)
 
         offsets = keep.tile([P, S // 16], U16, name="offsets")
         ts_window = sbuf("ts_window", [P, T], F32)
         scale_window = sbuf("scale_window", [P, T // 4], I32)
-        w_bf16 = [sbuf(f"w_bf16_{a}", [P, M, 4], BF16) for a in range(PASSES)]
         ts_picked = sbuf("ts_picked", [P, S], F32)
-        ts_cols = [sbuf(f"ts_cols{half}", [P, 4], F32) for half in range(2)]
-        ts_rows = sbuf("ts_rows", [P, HALF], F32)
-        bias = sbuf("bias", [P, 2], F32)
+        ts_rows = sbuf("ts_rows", [P, S], F32)
         ident = sbuf("ident", [P, P], F32)
         warm_in = sbuf("warm_in", [P, 1], F32)
         warm_out = sbuf("warm_out", [P, 1], F32)
-        banks = [psum.tile([P, 512], F32, name=f"bank{i}") for i in range(8)]
+        banks = [psum.tile([P, BANK], F32, name=f"bank{i}") for i in range(8)]
 
-        def listed(lo, hi):
-            return offsets[:, lo // 16 : hi // 16]
-
-        def load_words(a, buffer=None):
-            window = sbuf(f"word_window{a}", [P, T], I32, buffer)
+        def load_words(a, window):
             nc.sync.dma_start(out=window[:], in_=tab_words[a].rearrange("p t i -> p (t i)").bitcast(I32))
-            return window
 
         def load_w(a, raw):
-            nc.sync.dma_start(out=raw, in_=w[512 * a : 512 * (a + 1), :].rearrange("(p i) n -> p i n", i=4))
+            nc.sync.dma_start(out=raw[:], in_=w[512 * a : 512 * (a + 1), :].rearrange("(p i) n -> p i n", i=4))
 
         nc.sync.dma_start(offsets[:], offs)
         nc.sync.dma_start(out=ts_window[TS_ROW:P, :], in_=ts[0:1, :])
@@ -63,136 +62,117 @@ def tile_list_tabts_silu_kernel(tc, tab_words, tab_scales, w, ts, b, offs, out):
         nc.vector.memset(warm_in[:], 0.0)
         nc.vector.memset(ts_window[0:TS_ROW, :], 0.0)
         nc.scalar.activation(out=warm_out[:], in_=warm_in[:], func=ACT.Silu)
-        make_identity(nc, ident[:])
-        window0 = load_words(0)
-        w_first = sbuf("w_first", [P, 4, M], F32)
-        load_w(0, w_first[:])
-        b_rows = sbuf("b_rows", [P, P], F32)
-        nc.gpsimd.memset(b_rows[0 : P - 2, :], 0.0)
-        nc.sync.dma_start(out=b_rows[P - 2 : P, :], in_=b.rearrange("(h p) -> h p", p=P))
-        nc.tensor.transpose(banks[4][:, 0:P], b_rows[:], ident[:])
-        nc.scalar.copy(out=bias[:], in_=banks[4][:, P - 2 : P])
+        zeros = placed(late, "zeros", [P, (2 * WORD_BYTES + 2 * RAW_BYTES) // 4 + 16], F32, 0)
+        nc.gpsimd.memset(zeros[:, 0:P], 0.0)
+        nc.gpsimd.affine_select(
+            out=ident[:], in_=zeros[:, 0:P], compare_op=ALU.not_equal,
+            fill=1.0, base=0, pattern=[[-1, P]], channel_multiplier=1,
+        )
+
+        windows = [
+            placed(first_words, "word_window0", [P, T], I32, 0),
+            placed(late, "word_window1", [P, T], I32, 0),
+            placed(late, "word_window2", [P, T], I32, WORD_BYTES + RAW_BYTES),
+        ]
+        w_raw = [
+            placed(first_weights, "w_raw0", [P, 4, M], F32, 0),
+            placed(late, "w_raw1", [P, 4, M], F32, WORD_BYTES),
+            placed(late, "w_raw2", [P, 4, M], F32, 2 * WORD_BYTES + RAW_BYTES),
+        ]
+        bias = placed(late, "bias", [P, 2], F32, 2 * WORD_BYTES + 2 * RAW_BYTES)
+        load_words(0, windows[0])
+        load_w(0, w_raw[0])
         for q in range(4):
             nc.sync.dma_start(
                 out=scale_window[32 * q : 32 * q + 4 * PASSES, :],
                 in_=tab_scales[:, 4 * q : 4 * q + 4, :].bitcast(I32),
             )
-        w_rest = sbuf("w_rest", [P, 2, 4, M], F32, "warm_in")
-        w_raw = [w_first[:], w_rest[:, 0], w_rest[:, 1]]
-        load_w(1, w_raw[1])
-        window1 = load_words(1, "warm_out")
-        load_w(2, w_raw[2])
+        for a in range(1, PASSES):
+            load_words(a, windows[a])
+            load_w(a, w_raw[a])
+        with nc.allow_non_contiguous_dma(reason="one bias value a partition"):
+            nc.sync.dma_start(out=bias[:], in_=b.rearrange("(h p) -> p h", p=P))
 
-        nc.vector.tensor_copy(out=ts_picked[:], in_=ts_window[:].indirect(listed(0, S)))
-        window2 = load_words(2, "ts_window")
-        for half in (1, 0):
-            for u in range(4):
-                j0 = (4 * half + u) * P
-                nc.tensor.transpose(banks[5 + half][:, u * P : (u + 1) * P], ts_picked[:, j0 : j0 + P], ident[:])
+        def gather(picked, window):
+            nc.vector.tensor_copy(out=picked[:], in_=window.indirect(offsets[:]))
+
+        w_codes, w_scales, rounded = {}, {}, {}
+
+        def round_w(a, lo, hi):
+            rounded[a, lo] = sbuf(f"w_bf16_{a}_{lo}", [P, hi - lo, 4], BF16)
             nc.scalar.copy(
-                out=ts_cols[half][:],
-                in_=banks[5 + half][:].rearrange("p (u c) -> p u c", c=P)[:, :, TS_ROW],
+                out=rounded[a, lo][:].rearrange("p (c j) i -> p c i j", j=4),
+                in_=w_raw[a][:, :, lo:hi].rearrange("p i (c j) -> p c i j", j=4),
             )
-        for u in range(4):
-            nc.tensor.transpose(banks[7][:, u * P : (u + 1) * P], ts_cols[1][:, u : u + 1].to_broadcast([P, P]), ident[:])
-        nc.scalar.copy(out=ts_rows[:], in_=banks[7][:])
-        for a in range(PASSES):
-            nc.scalar.copy(out=w_bf16[a][:], in_=w_raw[a].rearrange("p i n -> p n i"))
+
+        def quantize_w(a, lo, hi, codes, scales):
+            nc.vector.quantize_mx(
+                out=codes[:].bitcast(FP8X4), scales=scales[:], in_=rounded[a, lo][:].rearrange("p n i -> p (n i)")
+            )
+            for n in range(lo, hi, P):
+                w_codes[a, n // P] = codes[:, n - lo : n - lo + P]
+                w_scales[a, n // P] = scales[:, n - lo : n - lo + P]
+
+        gather(ts_picked, ts_window[:])
+        round_w(0, 0, M)
+        ts_cols = placed(first_weights, "ts_cols", [P, (RAW_BYTES + M) // 4], F32, 0)
+        for u in range(8):
+            nc.tensor.transpose(banks[6 + u // 4][:, u % 4 * P : (u % 4 + 1) * P], ts_picked[:, u * P : (u + 1) * P], ident[:])
+        for half in range(2):
+            nc.scalar.copy(
+                out=ts_cols[:, 4 * half : 4 * half + 4],
+                in_=banks[6 + half][:].rearrange("p (u c) -> p u c", c=P)[:, :, TS_ROW],
+            )
+        for u in range(8):
+            column = ts_cols[:, u : u + 1].to_broadcast([P, P])
+            nc.tensor.transpose(banks[4 + u // 4][:, u % 4 * P : (u % 4 + 1) * P], column, ident[:])
+        for half in range(2):
+            nc.scalar.copy(out=ts_rows[:, half * BANK : (half + 1) * BANK], in_=banks[4 + half][:])
 
         v_codes = {}
 
-        def gather_words(a, window, lo, hi, buffer=None, step=None):
-            codes = sbuf(f"v_codes{a}_{lo}", [P, hi - lo], U32, buffer)
-            for s in range(lo // SLICE, hi // SLICE):
-                v_codes[a, s] = codes[:, s * SLICE - lo : (s + 1) * SLICE - lo]
-            for c in range(lo, hi, step or hi - lo):
-                c1 = c + (step or hi - lo)
-                nc.vector.tensor_copy(out=codes[:, c - lo : c1 - lo], in_=window[:].bitcast(U32).indirect(listed(c, c1)))
+        def matmuls(a, sums):
+            for i in sums:
+                h, lo, hi = SUMS[i]
+                nc.tensor.matmul_mx(
+                    out=banks[i][:, 0 : hi - lo],
+                    lhsT=w_codes[a, h].bitcast(FP8X4), lhsT_scale=w_scales[a, h],
+                    rhs=v_codes[a][:, lo:hi].bitcast(FP8X4), rhs_scale=v_scales[4 * a : P, lo:hi],
+                    start=(a == 0), stop=(a == PASSES - 1),
+                )
 
-        w_codes, w_scales = {}, {}
+        every_sum = range(len(SUMS))
+        v_codes[0] = sbuf("v_codes0", [P, S], U32)
+        gather(v_codes[0], windows[0][:].bitcast(U32))
+        v_scales = placed(first_words, "v_scales", [P, S], U8, 0)
+        gather(v_scales, scale_window[:].bitcast(U8))
+        quantize_w(
+            0, 0, M,
+            placed(first_words, "w_codes0", [P, M], U32, S),
+            placed(first_weights, "w_scales0", [P, M], U8, RAW_BYTES),
+        )
+        matmuls(0, every_sum)
 
-        def quantize_w(a, codes_buffer=None, scales_buffer=None):
-            w_codes[a] = sbuf(f"w_codes{a}", [P, M], U32, codes_buffer)
-            w_scales[a] = sbuf(f"w_scales{a}", [P, M], U8, scales_buffer)
-            nc.vector.quantize_mx(
-                out=w_codes[a][:].bitcast(FP8X4),
-                scales=w_scales[a][:],
-                in_=w_bf16[a][:].rearrange("p n i -> p (n i)"),
-            )
+        v_codes[1] = placed(first_weights, "v_codes1", [P, S], U32, 0)
+        gather(v_codes[1], windows[1][:].bitcast(U32))
+        round_w(1, 0, M)
+        quantize_w(1, 0, M, sbuf("w_codes1", [P, M], U32), sbuf("w_scales1", [P, M], U8))
+        matmuls(1, every_sum)
 
-        def matmuls(s, a):
-            flags = dict(start=(a == 0), stop=(a == PASSES - 1))
-            for h in range(2):
-                acc = banks[2 * s + h][:, 0:256]
-                part = slice(h * P, (h + 1) * P)
-                v_plane = v_scales[4 * a : P, s * SLICE : (s + 1) * SLICE]
-                if s < 2:
-                    nc.tensor.matmul_mx(
-                        out=acc,
-                        lhsT=v_codes[a, s][:, part].bitcast(FP8X4), lhsT_scale=v_plane[:, part],
-                        rhs=w_codes[a][:].bitcast(FP8X4), rhs_scale=w_scales[a][:],
-                        **flags,
-                    )
-                else:
-                    nc.tensor.matmul_mx(
-                        out=acc,
-                        lhsT=w_codes[a][:, part].bitcast(FP8X4), lhsT_scale=w_scales[a][:, part],
-                        rhs=v_codes[a, s].bitcast(FP8X4), rhs_scale=v_plane,
-                        **flags,
-                    )
+        v_codes[2] = placed(late, "v_codes2", [P, S], U32, WORD_BYTES)
+        gather(v_codes[2], windows[2][:].bitcast(U32))
+        for h in range(2):
+            round_w(2, h * P, (h + 1) * P)
+            quantize_w(2, h * P, (h + 1) * P, sbuf(f"w_codes2_{h}", [P, P], U32), sbuf(f"w_scales2_{h}", [P, P], U8))
+        matmuls(2, every_sum)
 
-        scaled = [[sbuf(f"scaled{s}_{h}", [P, SLICE], F32) for h in range(2)] for s in range(4)]
-        result = [[sbuf(f"result{s}_{h}", [P, SLICE], F32) for h in range(2)] for s in range(4)]
-
-        def scale(s):
-            for h in range(2):
-                acc = banks[2 * s + h][:, 0:256]
-                if s < 2:
-                    t = 2 * s + h
-                    nc.scalar.activation(out=scaled[s][h][:], in_=acc, func=ACT.Copy, scale=ts_cols[0][:, t : t + 1])
-                else:
-                    c0 = s * SLICE - HALF
-                    nc.vector.tensor_tensor(out=scaled[s][h][:], in0=acc, in1=ts_rows[:, c0 : c0 + SLICE], op=MULT)
-
-        def turn_back(s):
-            for h in range(2):
-                for u in range(2):
-                    nc.tensor.transpose(
-                        banks[2 * s + h][:, 256 + u * P : 256 + (u + 1) * P],
-                        scaled[s][u][:, h * P : (h + 1) * P],
-                        ident[:],
-                    )
-
-        def finish(s):
-            for h in range(2):
-                pre = banks[2 * s + h][:, 256:512] if s < 2 else scaled[s][h][:]
-                nc.scalar.activation(out=result[s][h][:], in_=pre, func=ACT.Silu, bias=bias[:, h : h + 1])
-                nc.sync.dma_start(out=out[h * P : (h + 1) * P, s * SLICE : (s + 1) * SLICE], in_=result[s][h][:])
-
-        gather_words(0, window0, 0, S)
-        v_scales = sbuf("v_scales", [P, S], U8, "word_window0")
-        nc.vector.tensor_copy(out=v_scales[:], in_=scale_window[:].bitcast(U8).indirect(listed(0, S)))
-        quantize_w(0, "scale_window", "ts_cols1")
-        for s in range(4):
-            matmuls(s, 0)
-        gather_words(1, window1, 0, HALF, "w_bf16_0")
-        quantize_w(1)
-        for s in range(2):
-            matmuls(s, 1)
-        gather_words(1, window1, HALF, S, "w_bf16_1")
-        quantize_w(2)
-        for s in range(2, 4):
-            matmuls(s, 1)
-        gather_words(2, window2, 0, S, "w_bf16_2", SLICE)
-        for s in range(2):
-            matmuls(s, 2)
-            scale(s)
-        turn_back(0)
-        matmuls(2, 2)
-        turn_back(1)
-        matmuls(3, 2)
-        finish(0)
-        finish(1)
-        for s in range(2, 4):
-            scale(s)
-            finish(s)
+        for i, (h, lo, hi) in enumerate(SUMS):
+            scaled = sbuf(f"scaled{i}", [P, hi - lo], F32)
+            nc.vector.tensor_tensor(out=scaled[:], in0=banks[i][:, 0 : hi - lo], in1=ts_rows[:, lo:hi], op=ALU.mult)
+            step = 256
+            for c in range(lo, hi, step):
+                result = sbuf(f"result{i}_{c}", [P, step], F32)
+                nc.scalar.activation(
+                    out=result[:], in_=scaled[:, c - lo : c - lo + step], func=ACT.Silu, bias=bias[:, h : h + 1]
+                )
+                nc.sync.dma_start(out=out[h * P : (h + 1) * P, c : c + step], in_=result[:])

@@ -22,7 +22,7 @@ BANK = 512
 TS_ROW = P - 1
 RAW_BYTES = 4 * M * 4
 WORD_BYTES = 4 * T
-SUMS = [(0, 0, 256), (0, 256, 512), (0, 512, 1024), (1, 0, 512), (1, 512, 768), (1, 768, 1024)]
+SUMS = [(h, lo, lo + 256) for h in range(2) for lo in range(0, S, 256)]
 
 
 def tile_list_tabts_silu_kernel(tc, tab_words, tab_scales, w, ts, b, offs, out):
@@ -32,6 +32,7 @@ def tile_list_tabts_silu_kernel(tc, tab_words, tab_scales, w, ts, b, offs, out):
         late = ctx.enter_context(tc.tile_pool(name="late", bufs=1))
         first_words = ctx.enter_context(tc.tile_pool(name="first_words", bufs=1))
         first_weights = ctx.enter_context(tc.tile_pool(name="first_weights", bufs=1))
+        picked_ts = ctx.enter_context(tc.tile_pool(name="picked_ts", bufs=1))
         psum = ctx.enter_context(tc.psum_pool(name="psum", bufs=1))
 
         def sbuf(name, shape, dtype):
@@ -43,7 +44,7 @@ def tile_list_tabts_silu_kernel(tc, tab_words, tab_scales, w, ts, b, offs, out):
         offsets = keep.tile([P, S // 16], U16, name="offsets")
         ts_window = sbuf("ts_window", [P, T], F32)
         scale_window = sbuf("scale_window", [P, T // 4], I32)
-        ts_picked = sbuf("ts_picked", [P, S], F32)
+        ts_picked = placed(picked_ts, "ts_picked", [P, S], F32, 0)
         ts_rows = sbuf("ts_rows", [P, S], F32)
         ident = sbuf("ident", [P, P], F32)
         warm_in = sbuf("warm_in", [P, 1], F32)
@@ -144,7 +145,7 @@ def tile_list_tabts_silu_kernel(tc, tab_words, tab_scales, w, ts, b, offs, out):
         every_sum = range(len(SUMS))
         v_codes[0] = sbuf("v_codes0", [P, S], U32)
         gather(v_codes[0], windows[0][:].bitcast(U32))
-        v_scales = placed(first_words, "v_scales", [P, S], U8, 0)
+        v_scales = placed(picked_ts, "v_scales", [P, S], U8, 0)
         gather(v_scales, scale_window[:].bitcast(U8))
         quantize_w(
             0, 0, M,

@@ -17,12 +17,17 @@ ACT = mybir.ActivationFunctionType
 ALU = mybir.AluOpType
 
 P = 128
-PASSES = K // 512
+PACK = 4
+K_PASS = P * PACK
+PASSES = K // K_PASS
+QUADRANTS = 4
 BANK = 512
+HALVES = M // P
 TS_ROW = P - 1
-RAW_BYTES = 4 * M * 4
+RAW_BYTES = PACK * M * 4
 WORD_BYTES = 4 * T
-SUMS = [(h, lo, lo + 256) for h in range(2) for lo in range(0, S, 256)]
+TOKENS = 256
+SUMS = [(h, lo) for h in range(HALVES) for lo in range(0, S, TOKENS)]
 
 
 def tile_list_tabts_silu_kernel(tc, tab_words, tab_scales, w, ts, b, offs, out):
@@ -47,22 +52,20 @@ def tile_list_tabts_silu_kernel(tc, tab_words, tab_scales, w, ts, b, offs, out):
         ts_picked = placed(picked_ts, "ts_picked", [P, S], F32, 0)
         ts_rows = sbuf("ts_rows", [P, S], F32)
         ident = sbuf("ident", [P, P], F32)
-        warm_in = sbuf("warm_in", [P, 1], F32)
-        warm_out = sbuf("warm_out", [P, 1], F32)
-        banks = [psum.tile([P, BANK], F32, name=f"bank{i}") for i in range(8)]
+        banks = [psum.tile([P, BANK], F32, name=f"bank{i}") for i in range(len(SUMS))]
 
         def load_words(a, window):
             nc.sync.dma_start(out=window[:], in_=tab_words[a].rearrange("p t i -> p (t i)").bitcast(I32))
 
         def load_w(a, raw):
-            nc.sync.dma_start(out=raw[:], in_=w[512 * a : 512 * (a + 1), :].rearrange("(p i) n -> p i n", i=4))
+            rows = w[K_PASS * a : K_PASS * (a + 1), :]
+            nc.sync.dma_start(out=raw[:], in_=rows.rearrange("(p i) n -> p i n", i=PACK))
 
         nc.sync.dma_start(offsets[:], offs)
         nc.sync.dma_start(out=ts_window[TS_ROW:P, :], in_=ts[0:1, :])
         nc.gpsimd.memset(scale_window[:], 0)
-        nc.vector.memset(warm_in[:], 0.0)
         nc.vector.memset(ts_window[0:TS_ROW, :], 0.0)
-        nc.scalar.activation(out=warm_out[:], in_=warm_in[:], func=ACT.Silu)
+
         zeros = placed(late, "zeros", [P, (2 * WORD_BYTES + 2 * RAW_BYTES) // 4 + 16], F32, 0)
         nc.gpsimd.memset(zeros[:, 0:P], 0.0)
         nc.gpsimd.affine_select(
@@ -76,14 +79,15 @@ def tile_list_tabts_silu_kernel(tc, tab_words, tab_scales, w, ts, b, offs, out):
             placed(late, "word_window2", [P, T], I32, WORD_BYTES + RAW_BYTES),
         ]
         w_raw = [
-            placed(first_weights, "w_raw0", [P, 4, M], F32, 0),
-            placed(late, "w_raw1", [P, 4, M], F32, WORD_BYTES),
-            placed(late, "w_raw2", [P, 4, M], F32, 2 * WORD_BYTES + RAW_BYTES),
+            placed(first_weights, "w_raw0", [P, PACK, M], F32, 0),
+            placed(late, "w_raw1", [P, PACK, M], F32, WORD_BYTES),
+            placed(late, "w_raw2", [P, PACK, M], F32, 2 * WORD_BYTES + RAW_BYTES),
         ]
-        bias = placed(late, "bias", [P, 2], F32, 2 * WORD_BYTES + 2 * RAW_BYTES)
+        bias = placed(late, "bias", [P, HALVES], F32, 2 * WORD_BYTES + 2 * RAW_BYTES)
+
         load_words(0, windows[0])
         load_w(0, w_raw[0])
-        for q in range(4):
+        for q in range(QUADRANTS):
             nc.sync.dma_start(
                 out=scale_window[32 * q : 32 * q + 4 * PASSES, :],
                 in_=tab_scales[:, 4 * q : 4 * q + 4, :].bitcast(I32),
@@ -100,7 +104,7 @@ def tile_list_tabts_silu_kernel(tc, tab_words, tab_scales, w, ts, b, offs, out):
         w_codes, w_scales, rounded = {}, {}, {}
 
         def round_w(a, lo, hi):
-            rounded[a, lo] = sbuf(f"w_bf16_{a}_{lo}", [P, hi - lo, 4], BF16)
+            rounded[a, lo] = sbuf(f"w_bf16_{a}_{lo}", [P, hi - lo, PACK], BF16)
             nc.scalar.copy(
                 out=rounded[a, lo][:].rearrange("p (c j) i -> p c i j", j=4),
                 in_=w_raw[a][:, :, lo:hi].rearrange("p i (c j) -> p c i j", j=4),
@@ -116,35 +120,37 @@ def tile_list_tabts_silu_kernel(tc, tab_words, tab_scales, w, ts, b, offs, out):
 
         gather(ts_picked, ts_window[:])
         round_w(0, 0, M)
+
+        blocks = S // P
+        per_bank = BANK // P
+        turned, spread = banks[6:8], banks[4:6]
         ts_cols = placed(first_weights, "ts_cols", [P, (RAW_BYTES + M) // 4], F32, 0)
-        for u in range(8):
-            nc.tensor.transpose(banks[6 + u // 4][:, u % 4 * P : (u % 4 + 1) * P], ts_picked[:, u * P : (u + 1) * P], ident[:])
-        for half in range(2):
+        for u in range(blocks):
+            place = slice(u % per_bank * P, (u % per_bank + 1) * P)
+            nc.tensor.transpose(turned[u // per_bank][:, place], ts_picked[:, u * P : (u + 1) * P], ident[:])
+        for i, bank in enumerate(turned):
             nc.scalar.copy(
-                out=ts_cols[:, 4 * half : 4 * half + 4],
-                in_=banks[6 + half][:].rearrange("p (u c) -> p u c", c=P)[:, :, TS_ROW],
+                out=ts_cols[:, per_bank * i : per_bank * (i + 1)],
+                in_=bank[:].rearrange("p (u c) -> p u c", c=P)[:, :, TS_ROW],
             )
-        for u in range(8):
-            column = ts_cols[:, u : u + 1].to_broadcast([P, P])
-            nc.tensor.transpose(banks[4 + u // 4][:, u % 4 * P : (u % 4 + 1) * P], column, ident[:])
-        for half in range(2):
-            nc.scalar.copy(out=ts_rows[:, half * BANK : (half + 1) * BANK], in_=banks[4 + half][:])
+        for u in range(blocks):
+            place = slice(u % per_bank * P, (u % per_bank + 1) * P)
+            nc.tensor.transpose(spread[u // per_bank][:, place], ts_cols[:, u : u + 1].to_broadcast([P, P]), ident[:])
+        for i, bank in enumerate(spread):
+            nc.scalar.copy(out=ts_rows[:, i * BANK : (i + 1) * BANK], in_=bank[:])
 
-        v_codes = {}
-
-        def matmuls(a, sums):
-            for i in sums:
-                h, lo, hi = SUMS[i]
+        def matmuls(a, v_codes):
+            for bank, (h, lo) in zip(banks, SUMS):
                 nc.tensor.matmul_mx(
-                    out=banks[i][:, 0 : hi - lo],
+                    out=bank[:, 0:TOKENS],
                     lhsT=w_codes[a, h].bitcast(FP8X4), lhsT_scale=w_scales[a, h],
-                    rhs=v_codes[a][:, lo:hi].bitcast(FP8X4), rhs_scale=v_scales[4 * a : P, lo:hi],
+                    rhs=v_codes[:, lo : lo + TOKENS].bitcast(FP8X4),
+                    rhs_scale=v_scales[4 * a : P, lo : lo + TOKENS],
                     start=(a == 0), stop=(a == PASSES - 1),
                 )
 
-        every_sum = range(len(SUMS))
-        v_codes[0] = sbuf("v_codes0", [P, S], U32)
-        gather(v_codes[0], windows[0][:].bitcast(U32))
+        v_codes0 = sbuf("v_codes0", [P, S], U32)
+        gather(v_codes0, windows[0][:].bitcast(U32))
         v_scales = placed(picked_ts, "v_scales", [P, S], U8, 0)
         gather(v_scales, scale_window[:].bitcast(U8))
         quantize_w(
@@ -152,28 +158,26 @@ def tile_list_tabts_silu_kernel(tc, tab_words, tab_scales, w, ts, b, offs, out):
             placed(first_words, "w_codes0", [P, M], U32, S),
             placed(first_weights, "w_scales0", [P, M], U8, RAW_BYTES),
         )
-        matmuls(0, every_sum)
+        matmuls(0, v_codes0)
 
-        v_codes[1] = placed(first_weights, "v_codes1", [P, S], U32, 0)
-        gather(v_codes[1], windows[1][:].bitcast(U32))
+        v_codes1 = placed(first_weights, "v_codes1", [P, S], U32, 0)
+        gather(v_codes1, windows[1][:].bitcast(U32))
         round_w(1, 0, M)
         quantize_w(1, 0, M, sbuf("w_codes1", [P, M], U32), sbuf("w_scales1", [P, M], U8))
-        matmuls(1, every_sum)
+        matmuls(1, v_codes1)
 
-        v_codes[2] = placed(late, "v_codes2", [P, S], U32, WORD_BYTES)
-        gather(v_codes[2], windows[2][:].bitcast(U32))
-        for h in range(2):
+        v_codes2 = placed(late, "v_codes2", [P, S], U32, WORD_BYTES)
+        gather(v_codes2, windows[2][:].bitcast(U32))
+        for h in range(HALVES):
             round_w(2, h * P, (h + 1) * P)
             quantize_w(2, h * P, (h + 1) * P, sbuf(f"w_codes2_{h}", [P, P], U32), sbuf(f"w_scales2_{h}", [P, P], U8))
-        matmuls(2, every_sum)
+        matmuls(2, v_codes2)
 
-        for i, (h, lo, hi) in enumerate(SUMS):
-            scaled = sbuf(f"scaled{i}", [P, hi - lo], F32)
-            nc.vector.tensor_tensor(out=scaled[:], in0=banks[i][:, 0 : hi - lo], in1=ts_rows[:, lo:hi], op=ALU.mult)
-            step = 256
-            for c in range(lo, hi, step):
-                result = sbuf(f"result{i}_{c}", [P, step], F32)
-                nc.scalar.activation(
-                    out=result[:], in_=scaled[:, c - lo : c - lo + step], func=ACT.Silu, bias=bias[:, h : h + 1]
-                )
-                nc.sync.dma_start(out=out[h * P : (h + 1) * P, c : c + step], in_=result[:])
+        for i, (h, lo) in enumerate(SUMS):
+            scaled = sbuf(f"scaled{i}", [P, TOKENS], F32)
+            nc.vector.tensor_tensor(
+                out=scaled[:], in0=banks[i][:, 0:TOKENS], in1=ts_rows[:, lo : lo + TOKENS], op=ALU.mult
+            )
+            result = sbuf(f"result{i}", [P, TOKENS], F32)
+            nc.scalar.activation(out=result[:], in_=scaled[:], func=ACT.Silu, bias=bias[:, h : h + 1])
+            nc.sync.dma_start(out=out[h * P : (h + 1) * P, lo : lo + TOKENS], in_=result[:])

@@ -27,7 +27,7 @@ TS_ROW = P - 1
 RAW_BYTES = PACK * M * 4
 WORD_BYTES = 4 * T
 TOKENS = 256
-SUMS = [(h, lo) for h in range(HALVES) for lo in range(0, S, TOKENS)]
+SUMS = [(h, lo) for lo in range(0, S, TOKENS) for h in range(HALVES)]
 
 
 def tile_list_tabts_silu_kernel(tc, tab_words, tab_scales, w, ts, b, offs, out):
@@ -98,8 +98,8 @@ def tile_list_tabts_silu_kernel(tc, tab_words, tab_scales, w, ts, b, offs, out):
         with nc.allow_non_contiguous_dma(reason="one bias value a partition"):
             nc.sync.dma_start(out=bias[:], in_=b.rearrange("(h p) -> p h", p=P))
 
-        def gather(picked, window):
-            nc.vector.tensor_copy(out=picked[:], in_=window.indirect(offsets[:]))
+        def gather(picked, window, lo=0, hi=S):
+            nc.vector.tensor_copy(out=picked[:], in_=window.indirect(offsets[:, lo // 16 : hi // 16]))
 
         w_codes, w_scales, rounded = {}, {}, {}
 
@@ -139,12 +139,14 @@ def tile_list_tabts_silu_kernel(tc, tab_words, tab_scales, w, ts, b, offs, out):
         for i, bank in enumerate(spread):
             nc.scalar.copy(out=ts_rows[:, i * BANK : (i + 1) * BANK], in_=bank[:])
 
-        def matmuls(a, v_codes):
+        def matmuls(a, v_codes, first=0, last=S):
             for bank, (h, lo) in zip(banks, SUMS):
+                if not first <= lo < last:
+                    continue
                 nc.tensor.matmul_mx(
                     out=bank[:, 0:TOKENS],
                     lhsT=w_codes[a, h].bitcast(FP8X4), lhsT_scale=w_scales[a, h],
-                    rhs=v_codes[:, lo : lo + TOKENS].bitcast(FP8X4),
+                    rhs=v_codes[:, lo - first : lo - first + TOKENS].bitcast(FP8X4),
                     rhs_scale=v_scales[4 * a : P, lo : lo + TOKENS],
                     start=(a == 0), stop=(a == PASSES - 1),
                 )
@@ -160,24 +162,45 @@ def tile_list_tabts_silu_kernel(tc, tab_words, tab_scales, w, ts, b, offs, out):
         )
         matmuls(0, v_codes0)
 
-        v_codes1 = placed(first_weights, "v_codes1", [P, S], U32, 0)
-        gather(v_codes1, windows[1][:].bitcast(U32))
+        window1 = windows[1][:].bitcast(U32)
+        v_low1 = placed(first_weights, "v_low1", [P, S // 2], U32, 0)
+        gather(v_low1, window1, 0, S // 2)
         round_w(1, 0, M)
         quantize_w(1, 0, M, sbuf("w_codes1", [P, M], U32), sbuf("w_scales1", [P, M], U8))
-        matmuls(1, v_codes1)
+        matmuls(1, v_low1, 0, S // 2)
+        v_high1 = placed(late, "v_high1", [P, S // 2], U32, WORD_BYTES + 2 * S)
+        gather(v_high1, window1, S // 2, S)
+        matmuls(1, v_high1, S // 2, S)
 
-        v_codes2 = placed(late, "v_codes2", [P, S], U32, WORD_BYTES)
-        gather(v_codes2, windows[2][:].bitcast(U32))
+        window2 = windows[2][:].bitcast(U32)
+        v_front = placed(late, "v_front", [P, 2 * TOKENS], U32, WORD_BYTES)
+        gather(v_front, window2, 0, 2 * TOKENS)
         for h in range(HALVES):
             round_w(2, h * P, (h + 1) * P)
             quantize_w(2, h * P, (h + 1) * P, sbuf(f"w_codes2_{h}", [P, P], U32), sbuf(f"w_scales2_{h}", [P, P], U8))
-        matmuls(2, v_codes2)
+        matmuls(2, v_front, 0, 2 * TOKENS)
+        raw2 = 2 * WORD_BYTES + RAW_BYTES
+        v_third = placed(late, "v_third", [P, TOKENS], U32, raw2 + 4 * TOKENS)
+        gather(v_third, window2, 2 * TOKENS, 3 * TOKENS)
+        matmuls(2, v_third, 2 * TOKENS, 3 * TOKENS)
 
-        for i, (h, lo) in enumerate(SUMS):
-            scaled = sbuf(f"scaled{i}", [P, TOKENS], F32)
+        def finish(i):
+            h, lo = SUMS[i]
+            if i == 0:
+                scaled = placed(late, "scaled0", [P, TOKENS], F32, raw2)
+            else:
+                scaled = sbuf(f"scaled{i}", [P, TOKENS], F32)
             nc.vector.tensor_tensor(
                 out=scaled[:], in0=banks[i][:, 0:TOKENS], in1=ts_rows[:, lo : lo + TOKENS], op=ALU.mult
             )
             result = sbuf(f"result{i}", [P, TOKENS], F32)
             nc.scalar.activation(out=result[:], in_=scaled[:], func=ACT.Silu, bias=bias[:, h : h + 1])
             nc.sync.dma_start(out=out[h * P : (h + 1) * P, lo : lo + TOKENS], in_=result[:])
+
+        for i in range(HALVES):
+            finish(i)
+        v_last = placed(late, "v_last", [P, TOKENS], U32, raw2 + 8 * TOKENS)
+        gather(v_last, window2, 3 * TOKENS, S)
+        matmuls(2, v_last, 3 * TOKENS, S)
+        for i in range(HALVES, len(SUMS)):
+            finish(i)

@@ -50,7 +50,8 @@ def tile_list_tabts_silu_kernel(tc, tab_words, tab_scales, w, ts, b, offs, out):
         ts_window = sbuf("ts_window", [P, T], F32)
         scale_window = sbuf("scale_window", [P, T // 4], I32)
         ts_picked = placed(picked_ts, "ts_picked", [P, S], F32, 0)
-        ts_rows = sbuf("ts_rows", [P, S], F32)
+        ts_rows = sbuf("ts_rows", [P, S - TOKENS], F32)
+        ts_turned = sbuf("ts_turned", [P, HALVES], F32)
         ident = sbuf("ident", [P, P], F32)
         banks = [psum.tile([P, BANK], F32, name=f"bank{i}") for i in range(len(SUMS))]
 
@@ -92,16 +93,17 @@ def tile_list_tabts_silu_kernel(tc, tab_words, tab_scales, w, ts, b, offs, out):
                 out=scale_window[32 * q : 32 * q + 4 * PASSES, :],
                 in_=tab_scales[:, 4 * q : 4 * q + 4, :].bitcast(I32),
             )
-        for a in range(1, PASSES):
-            load_words(a, windows[a])
-            load_w(a, w_raw[a])
+        load_words(1, windows[1])
+        load_w(1, w_raw[1])
+        load_w(2, w_raw[2])
+        load_words(2, windows[2])
         with nc.allow_non_contiguous_dma(reason="one bias value a partition"):
             nc.sync.dma_start(out=bias[:], in_=b.rearrange("(h p) -> p h", p=P))
 
         def gather(picked, window, lo=0, hi=S):
             nc.vector.tensor_copy(out=picked[:], in_=window.indirect(offsets[:, lo // 16 : hi // 16]))
 
-        w_codes, w_scales, rounded = {}, {}, {}
+        w_codes, w_scales, w_whole, rounded = {}, {}, {}, {}
 
         def round_w(a, lo, hi):
             rounded[a, lo] = sbuf(f"w_bf16_{a}_{lo}", [P, hi - lo, PACK], BF16)
@@ -112,13 +114,17 @@ def tile_list_tabts_silu_kernel(tc, tab_words, tab_scales, w, ts, b, offs, out):
 
         def quantize_w(a, lo, hi, codes, scales):
             nc.vector.quantize_mx(
-                out=codes[:].bitcast(FP8X4), scales=scales[:], in_=rounded[a, lo][:].rearrange("p n i -> p (n i)")
+                out=codes[:, lo:hi].bitcast(FP8X4), scales=scales[:, lo:hi],
+                in_=rounded[a, lo][:].rearrange("p n i -> p (n i)"),
             )
+            w_whole[a] = (codes, scales)
             for n in range(lo, hi, P):
-                w_codes[a, n // P] = codes[:, n - lo : n - lo + P]
-                w_scales[a, n // P] = scales[:, n - lo : n - lo + P]
+                w_codes[a, n // P] = codes[:, n : n + P]
+                w_scales[a, n // P] = scales[:, n : n + P]
 
         gather(ts_picked, ts_window[:])
+        warm = sbuf("warm", [P, 1], F32)
+        nc.scalar.activation(out=warm[:], in_=w_raw[0][:, 0, 0:1], func=ACT.Silu)
         round_w(0, 0, M)
 
         blocks = S // P
@@ -133,15 +139,29 @@ def tile_list_tabts_silu_kernel(tc, tab_words, tab_scales, w, ts, b, offs, out):
                 out=ts_cols[:, per_bank * i : per_bank * (i + 1)],
                 in_=bank[:].rearrange("p (u c) -> p u c", c=P)[:, :, TS_ROW],
             )
-        for u in range(blocks):
+        nc.scalar.copy(
+            out=ts_turned[:], in_=turned[0][:].rearrange("p (u c) -> p u c", c=P)[:, 0:HALVES, TS_ROW]
+        )
+        for u in range(blocks - HALVES):
             place = slice(u % per_bank * P, (u % per_bank + 1) * P)
-            nc.tensor.transpose(spread[u // per_bank][:, place], ts_cols[:, u : u + 1].to_broadcast([P, P]), ident[:])
+            column = ts_cols[:, HALVES + u : HALVES + u + 1]
+            nc.tensor.transpose(spread[u // per_bank][:, place], column.to_broadcast([P, P]), ident[:])
         for i, bank in enumerate(spread):
-            nc.scalar.copy(out=ts_rows[:, i * BANK : (i + 1) * BANK], in_=bank[:])
+            width = min(BANK, S - TOKENS - i * BANK)
+            nc.scalar.copy(out=ts_rows[:, i * BANK : i * BANK + width], in_=bank[:, 0:width])
 
         def matmuls(a, v_codes, first=0, last=S):
             for bank, (h, lo) in zip(banks, SUMS):
                 if not first <= lo < last:
+                    continue
+                if lo == 0:
+                    nc.tensor.matmul_mx(
+                        out=bank[:, 0:M],
+                        lhsT=v_codes[:, h * P : (h + 1) * P].bitcast(FP8X4),
+                        lhsT_scale=v_scales[4 * a : P, h * P : (h + 1) * P],
+                        rhs=w_whole[a][0][:].bitcast(FP8X4), rhs_scale=w_whole[a][1][:],
+                        start=(a == 0), stop=(a == PASSES - 1),
+                    )
                     continue
                 nc.tensor.matmul_mx(
                     out=bank[:, 0:TOKENS],
@@ -162,45 +182,51 @@ def tile_list_tabts_silu_kernel(tc, tab_words, tab_scales, w, ts, b, offs, out):
         )
         matmuls(0, v_codes0)
 
-        window1 = windows[1][:].bitcast(U32)
-        v_low1 = placed(first_weights, "v_low1", [P, S // 2], U32, 0)
-        gather(v_low1, window1, 0, S // 2)
-        round_w(1, 0, M)
-        quantize_w(1, 0, M, sbuf("w_codes1", [P, M], U32), sbuf("w_scales1", [P, M], U8))
-        matmuls(1, v_low1, 0, S // 2)
-        v_high1 = placed(late, "v_high1", [P, S // 2], U32, WORD_BYTES + 2 * S)
-        gather(v_high1, window1, S // 2, S)
-        matmuls(1, v_high1, S // 2, S)
+        v_codes1 = placed(first_weights, "v_codes1", [P, S], U32, 0)
+        gather(v_codes1, windows[1][:].bitcast(U32))
+        for a in range(1, PASSES):
+            round_w(a, 0, M)
+            quantize_w(a, 0, M, sbuf(f"w_codes{a}", [P, M], U32), sbuf(f"w_scales{a}", [P, M], U8))
+        matmuls(1, v_codes1)
 
         window2 = windows[2][:].bitcast(U32)
-        v_front = placed(late, "v_front", [P, 2 * TOKENS], U32, WORD_BYTES)
-        gather(v_front, window2, 0, 2 * TOKENS)
-        for h in range(HALVES):
-            round_w(2, h * P, (h + 1) * P)
-            quantize_w(2, h * P, (h + 1) * P, sbuf(f"w_codes2_{h}", [P, P], U32), sbuf(f"w_scales2_{h}", [P, P], U8))
-        matmuls(2, v_front, 0, 2 * TOKENS)
         raw2 = 2 * WORD_BYTES + RAW_BYTES
-        v_third = placed(late, "v_third", [P, TOKENS], U32, raw2 + 4 * TOKENS)
-        gather(v_third, window2, 2 * TOKENS, 3 * TOKENS)
-        matmuls(2, v_third, 2 * TOKENS, 3 * TOKENS)
+        v_front = placed(late, "v_front", [P, S // 2], U32, raw2)
+        gather(v_front, window2, 0, S // 2)
+        matmuls(2, v_front, 0, S // 2)
+        v_back = placed(late, "v_back", [P, S // 2], U32, raw2 + 2 * S)
+        gather(v_back, window2, S // 2, S)
 
-        def finish(i):
+        results = [sbuf(f"result{i}", [P, TOKENS], F32) for i in range(len(SUMS))]
+
+        def store(i):
             h, lo = SUMS[i]
-            if i == 0:
-                scaled = placed(late, "scaled0", [P, TOKENS], F32, raw2)
-            else:
-                scaled = sbuf(f"scaled{i}", [P, TOKENS], F32)
-            nc.vector.tensor_tensor(
-                out=scaled[:], in0=banks[i][:, 0:TOKENS], in1=ts_rows[:, lo : lo + TOKENS], op=ALU.mult
-            )
-            result = sbuf(f"result{i}", [P, TOKENS], F32)
-            nc.scalar.activation(out=result[:], in_=scaled[:], func=ACT.Silu, bias=bias[:, h : h + 1])
-            nc.sync.dma_start(out=out[h * P : (h + 1) * P, lo : lo + TOKENS], in_=result[:])
+            nc.sync.dma_start(out=out[h * P : (h + 1) * P, lo : lo + TOKENS], in_=results[i][:])
 
-        for i in range(HALVES):
-            finish(i)
-        v_last = placed(late, "v_last", [P, TOKENS], U32, raw2 + 8 * TOKENS)
-        gather(v_last, window2, 3 * TOKENS, S)
-        matmuls(2, v_last, 3 * TOKENS, S)
+        def activate(result, scaled, h):
+            nc.scalar.activation(out=result, in_=scaled, func=ACT.Silu, bias=bias[:, h : h + 1])
+
+        by_token = []
+        for u in range(HALVES):
+            by_token.append(sbuf(f"by_token{u}", [P, M], F32))
+            nc.scalar.activation(
+                out=by_token[u][:], in_=banks[u][:, 0:M], func=ACT.Copy, scale=ts_turned[:, u : u + 1]
+            )
+        for u in range(HALVES):
+            for h in range(HALVES):
+                nc.tensor.transpose(banks[u][:, h * P : (h + 1) * P], by_token[u][:, h * P : (h + 1) * P], ident[:])
+        for u in range(HALVES):
+            for h in range(HALVES):
+                activate(results[h][:, u * P : (u + 1) * P], banks[u][:, h * P : (h + 1) * P], h)
+        for h in range(HALVES):
+            store(h)
+
+        matmuls(2, v_back, S // 2, S)
         for i in range(HALVES, len(SUMS)):
-            finish(i)
+            h, lo = SUMS[i]
+            scaled = sbuf(f"scaled{i}", [P, TOKENS], F32)
+            nc.vector.tensor_tensor(
+                out=scaled[:], in0=banks[i][:, 0:TOKENS], in1=ts_rows[:, lo - TOKENS : lo], op=ALU.mult
+            )
+            activate(results[i][:], scaled[:], h)
+            store(i)

@@ -27,6 +27,7 @@ TS_ROW = P - 1
 RAW_BYTES = PACK * M * 4
 WORD_BYTES = 4 * T
 TOKENS = 256
+TURNED = TOKENS // P
 SUMS = [(h, lo) for lo in range(0, S, TOKENS) for h in range(HALVES)]
 
 
@@ -38,6 +39,9 @@ def tile_list_tabts_silu_kernel(tc, tab_words, tab_scales, w, ts, b, offs, out):
         first_words = ctx.enter_context(tc.tile_pool(name="first_words", bufs=1))
         first_weights = ctx.enter_context(tc.tile_pool(name="first_weights", bufs=1))
         picked_ts = ctx.enter_context(tc.tile_pool(name="picked_ts", bufs=1))
+        early_rounded = ctx.enter_context(tc.tile_pool(name="early_rounded", bufs=1))
+        turned_ts = ctx.enter_context(tc.tile_pool(name="turned_ts", bufs=1))
+        last_turned = ctx.enter_context(tc.tile_pool(name="last_turned", bufs=1))
         psum = ctx.enter_context(tc.psum_pool(name="psum", bufs=1))
 
         def sbuf(name, shape, dtype):
@@ -50,24 +54,22 @@ def tile_list_tabts_silu_kernel(tc, tab_words, tab_scales, w, ts, b, offs, out):
         ts_window = sbuf("ts_window", [P, T], F32)
         scale_window = sbuf("scale_window", [P, T // 4], I32)
         ts_picked = placed(picked_ts, "ts_picked", [P, S], F32, 0)
-        ts_rows = sbuf("ts_rows", [P, S - TOKENS], F32)
-        ts_turned = sbuf("ts_turned", [P, HALVES], F32)
         ident = sbuf("ident", [P, P], F32)
         banks = [psum.tile([P, BANK], F32, name=f"bank{i}") for i in range(len(SUMS))]
 
         def load_words(a, window):
             nc.sync.dma_start(out=window[:], in_=tab_words[a].rearrange("p t i -> p (t i)").bitcast(I32))
 
-        def load_w(a, raw):
+        def load_w(a, raw, lo=0, hi=PACK):
             rows = w[K_PASS * a : K_PASS * (a + 1), :]
-            nc.sync.dma_start(out=raw[:], in_=rows.rearrange("(p i) n -> p i n", i=PACK))
+            nc.sync.dma_start(out=raw[:], in_=rows.rearrange("(p i) n -> p i n", i=PACK)[:, lo:hi, :])
 
         nc.sync.dma_start(offsets[:], offs)
-        nc.sync.dma_start(out=ts_window[TS_ROW:P, :], in_=ts[0:1, :])
+        nc.scalar.dma_start(out=ts_window[TS_ROW:P, :], in_=ts[0:1, :])
         nc.gpsimd.memset(scale_window[:], 0)
         nc.vector.memset(ts_window[0:TS_ROW, :], 0.0)
 
-        zeros = placed(late, "zeros", [P, (2 * WORD_BYTES + 2 * RAW_BYTES) // 4 + 16], F32, 0)
+        zeros = placed(late, "zeros", [P, (2 * WORD_BYTES + 3 * RAW_BYTES) // 4 + 16], F32, 0)
         nc.gpsimd.memset(zeros[:, 0:P], 0.0)
         nc.gpsimd.affine_select(
             out=ident[:], in_=zeros[:, 0:P], compare_op=ALU.not_equal,
@@ -77,14 +79,15 @@ def tile_list_tabts_silu_kernel(tc, tab_words, tab_scales, w, ts, b, offs, out):
         windows = [
             placed(first_words, "word_window0", [P, T], I32, 0),
             placed(late, "word_window1", [P, T], I32, 0),
-            placed(late, "word_window2", [P, T], I32, WORD_BYTES + RAW_BYTES),
+            placed(late, "word_window2", [P, T], I32, WORD_BYTES),
         ]
         w_raw = [
             placed(first_weights, "w_raw0", [P, PACK, M], F32, 0),
-            placed(late, "w_raw1", [P, PACK, M], F32, WORD_BYTES),
-            placed(late, "w_raw2", [P, PACK, M], F32, 2 * WORD_BYTES + RAW_BYTES),
+            placed(late, "w_raw1", [P, PACK, M], F32, 2 * WORD_BYTES + RAW_BYTES // 2),
         ]
-        bias = placed(late, "bias", [P, HALVES], F32, 2 * WORD_BYTES + 2 * RAW_BYTES)
+        raw2 = 2 * WORD_BYTES + 2 * RAW_BYTES
+        w_raw.append(placed(late, "w_raw2", [P, PACK, M], F32, raw2))
+        bias = placed(late, "bias", [P, HALVES], F32, 2 * WORD_BYTES + 3 * RAW_BYTES)
 
         load_words(0, windows[0])
         load_w(0, w_raw[0])
@@ -93,8 +96,8 @@ def tile_list_tabts_silu_kernel(tc, tab_words, tab_scales, w, ts, b, offs, out):
                 out=scale_window[32 * q : 32 * q + 4 * PASSES, :],
                 in_=tab_scales[:, 4 * q : 4 * q + 4, :].bitcast(I32),
             )
-        load_words(1, windows[1])
         load_w(1, w_raw[1])
+        load_words(1, windows[1])
         load_w(2, w_raw[2])
         load_words(2, windows[2])
         with nc.allow_non_contiguous_dma(reason="one bias value a partition"):
@@ -103,34 +106,35 @@ def tile_list_tabts_silu_kernel(tc, tab_words, tab_scales, w, ts, b, offs, out):
         def gather(picked, window, lo=0, hi=S):
             nc.vector.tensor_copy(out=picked[:], in_=window.indirect(offsets[:, lo // 16 : hi // 16]))
 
-        w_codes, w_scales, w_whole, rounded = {}, {}, {}, {}
+        w_codes, w_scales = {}, {}
 
-        def round_w(a, lo, hi):
-            rounded[a, lo] = sbuf(f"w_bf16_{a}_{lo}", [P, hi - lo, PACK], BF16)
+        def round_w(rounded, raw):
             nc.scalar.copy(
-                out=rounded[a, lo][:].rearrange("p (c j) i -> p c i j", j=4),
-                in_=w_raw[a][:, :, lo:hi].rearrange("p i (c j) -> p c i j", j=4),
+                out=rounded.rearrange("p (c j) i -> p c i j", j=4),
+                in_=raw.rearrange("p i (c j) -> p c i j", j=4),
             )
 
-        def quantize_w(a, lo, hi, codes, scales):
+        def quantize_w(rounded, groups, codes, scales):
             nc.vector.quantize_mx(
-                out=codes[:, lo:hi].bitcast(FP8X4), scales=scales[:, lo:hi],
-                in_=rounded[a, lo][:].rearrange("p n i -> p (n i)"),
+                out=codes[:].bitcast(FP8X4), scales=scales[:], in_=rounded.rearrange("p n i -> p (n i)")
             )
-            w_whole[a] = (codes, scales)
-            for n in range(lo, hi, P):
-                w_codes[a, n // P] = codes[:, n : n + P]
-                w_scales[a, n // P] = scales[:, n : n + P]
+            for j, group in enumerate(groups):
+                w_codes[group] = codes[:, j * P : (j + 1) * P]
+                w_scales[group] = scales[:, j * P : (j + 1) * P]
+                if group[1] == 0:
+                    w_codes[group[0]] = codes[:, j * P : j * P + M]
+                    w_scales[group[0]] = scales[:, j * P : j * P + M]
 
         gather(ts_picked, ts_window[:])
+        w_early = placed(early_rounded, "w_early", [P, 2 * M, PACK], BF16, 0)
         warm = sbuf("warm", [P, 1], F32)
         nc.scalar.activation(out=warm[:], in_=w_raw[0][:, 0, 0:1], func=ACT.Silu)
-        round_w(0, 0, M)
+        round_w(w_early[:, 0:M, :], w_raw[0][:])
 
         blocks = S // P
         per_bank = BANK // P
         turned, spread = banks[6:8], banks[4:6]
-        ts_cols = placed(first_weights, "ts_cols", [P, (RAW_BYTES + M) // 4], F32, 0)
+        ts_cols = placed(first_weights, "ts_cols", [P, RAW_BYTES // 4], F32, 0)
         for u in range(blocks):
             place = slice(u % per_bank * P, (u % per_bank + 1) * P)
             nc.tensor.transpose(turned[u // per_bank][:, place], ts_picked[:, u * P : (u + 1) * P], ident[:])
@@ -139,27 +143,29 @@ def tile_list_tabts_silu_kernel(tc, tab_words, tab_scales, w, ts, b, offs, out):
                 out=ts_cols[:, per_bank * i : per_bank * (i + 1)],
                 in_=bank[:].rearrange("p (u c) -> p u c", c=P)[:, :, TS_ROW],
             )
-        nc.scalar.copy(
-            out=ts_turned[:], in_=turned[0][:].rearrange("p (u c) -> p u c", c=P)[:, 0:HALVES, TS_ROW]
-        )
-        for u in range(blocks - HALVES):
+        ts_turned = [placed(turned_ts, "ts_turned0", [P, 1], F32, 0), sbuf("ts_turned1", [P, 1], F32)]
+        for u in range(TURNED):
+            nc.scalar.copy(out=ts_turned[u][:], in_=turned[0][:, u * P + TS_ROW : u * P + TS_ROW + 1])
+        round_w(w_early[:, M : 2 * M, :], w_raw[1][:])
+        for u in range(blocks - TURNED):
             place = slice(u % per_bank * P, (u % per_bank + 1) * P)
-            column = ts_cols[:, HALVES + u : HALVES + u + 1]
+            column = ts_cols[:, TURNED + u : TURNED + u + 1]
             nc.tensor.transpose(spread[u // per_bank][:, place], column.to_broadcast([P, P]), ident[:])
+        ts_rows = placed(late, "ts_rows", [P, S - TOKENS], F32, 2 * WORD_BYTES)
         for i, bank in enumerate(spread):
             width = min(BANK, S - TOKENS - i * BANK)
             nc.scalar.copy(out=ts_rows[:, i * BANK : i * BANK + width], in_=bank[:, 0:width])
 
-        def matmuls(a, v_codes, first=0, last=S):
+        def matmuls(a, v_codes, first, lo_sum, hi_sum, halves=range(HALVES), closing=PASSES - 1):
             for bank, (h, lo) in zip(banks, SUMS):
-                if not first <= lo < last:
+                if not (lo_sum <= lo < hi_sum and h in halves):
                     continue
                 if lo == 0:
                     nc.tensor.matmul_mx(
                         out=bank[:, 0:M],
                         lhsT=v_codes[:, h * P : (h + 1) * P].bitcast(FP8X4),
                         lhsT_scale=v_scales[4 * a : P, h * P : (h + 1) * P],
-                        rhs=w_whole[a][0][:].bitcast(FP8X4), rhs_scale=w_whole[a][1][:],
+                        rhs=w_codes[a].bitcast(FP8X4), rhs_scale=w_scales[a],
                         start=(a == 0), stop=(a == PASSES - 1),
                     )
                     continue
@@ -168,7 +174,7 @@ def tile_list_tabts_silu_kernel(tc, tab_words, tab_scales, w, ts, b, offs, out):
                     lhsT=w_codes[a, h].bitcast(FP8X4), lhsT_scale=w_scales[a, h],
                     rhs=v_codes[:, lo - first : lo - first + TOKENS].bitcast(FP8X4),
                     rhs_scale=v_scales[4 * a : P, lo : lo + TOKENS],
-                    start=(a == 0), stop=(a == PASSES - 1),
+                    start=(a == 0), stop=(a == closing),
                 )
 
         v_codes0 = sbuf("v_codes0", [P, S], U32)
@@ -176,28 +182,35 @@ def tile_list_tabts_silu_kernel(tc, tab_words, tab_scales, w, ts, b, offs, out):
         v_scales = placed(picked_ts, "v_scales", [P, S], U8, 0)
         gather(v_scales, scale_window[:].bitcast(U8))
         quantize_w(
-            0, 0, M,
-            placed(first_words, "w_codes0", [P, M], U32, S),
-            placed(first_weights, "w_scales0", [P, M], U8, RAW_BYTES),
+            w_early[:], [(a, h) for a in range(2) for h in range(HALVES)],
+            placed(first_words, "w_codes_early", [P, 2 * M], U32, S),
+            placed(first_weights, "w_scales_early", [P, 2 * M], U8, 0),
         )
-        matmuls(0, v_codes0)
+        matmuls(0, v_codes0, 0, 0, S)
 
-        v_codes1 = placed(first_weights, "v_codes1", [P, S], U32, 0)
+        v_codes1 = placed(late, "v_codes1", [P, S], U32, 2 * WORD_BYTES + RAW_BYTES)
         gather(v_codes1, windows[1][:].bitcast(U32))
-        for a in range(1, PASSES):
-            round_w(a, 0, M)
-            quantize_w(a, 0, M, sbuf(f"w_codes{a}", [P, M], U32), sbuf(f"w_scales{a}", [P, M], U8))
-        matmuls(1, v_codes1)
+        matmuls(1, v_codes1, 0, 0, S - TOKENS)
 
         window2 = windows[2][:].bitcast(U32)
-        raw2 = 2 * WORD_BYTES + RAW_BYTES
-        v_front = placed(late, "v_front", [P, S // 2], U32, raw2)
-        gather(v_front, window2, 0, S // 2)
-        matmuls(2, v_front, 0, S // 2)
+        w_late = sbuf("w_late", [P, M, PACK], BF16)
+        round_w(w_late[:], w_raw[2][:])
+        quantize_w(
+            w_late[:], [(2, h) for h in range(HALVES)],
+            placed(early_rounded, "w_codes2", [P, M], U32, 0), sbuf("w_scales2", [P, M], U8),
+        )
+        for lo in (0, TOKENS):
+            v_front = placed(late, f"v_front{lo}", [P, TOKENS], U32, raw2 + 4 * lo)
+            gather(v_front, window2, lo, lo + TOKENS)
+            matmuls(2, v_front, lo, lo, lo + TOKENS)
         v_back = placed(late, "v_back", [P, S // 2], U32, raw2 + 2 * S)
         gather(v_back, window2, S // 2, S)
 
-        results = [sbuf(f"result{i}", [P, TOKENS], F32) for i in range(len(SUMS))]
+        results = [sbuf(f"result{i}", [P, TOKENS], F32) for i in range(HALVES)]
+        results = results + [
+            placed(last_turned, f"result{i}", [P, TOKENS], F32, 4 * TOKENS * (i - HALVES))
+            for i in range(HALVES, len(SUMS))
+        ]
 
         def store(i):
             h, lo = SUMS[i]
@@ -206,22 +219,32 @@ def tile_list_tabts_silu_kernel(tc, tab_words, tab_scales, w, ts, b, offs, out):
         def activate(result, scaled, h):
             nc.scalar.activation(out=result, in_=scaled, func=ACT.Silu, bias=bias[:, h : h + 1])
 
-        by_token = []
-        for u in range(HALVES):
-            by_token.append(sbuf(f"by_token{u}", [P, M], F32))
+        by_token = [
+            sbuf("by_token0", [P, M], F32),
+            placed(last_turned, "by_token1", [P, TOKENS * (len(SUMS) - HALVES)], F32, 0),
+        ]
+        for u in range(TURNED):
             nc.scalar.activation(
-                out=by_token[u][:], in_=banks[u][:, 0:M], func=ACT.Copy, scale=ts_turned[:, u : u + 1]
+                out=by_token[u][:, 0:M], in_=banks[u][:, 0:M], func=ACT.Copy, scale=ts_turned[u][:]
             )
-        for u in range(HALVES):
+        for u in range(TURNED):
             for h in range(HALVES):
                 nc.tensor.transpose(banks[u][:, h * P : (h + 1) * P], by_token[u][:, h * P : (h + 1) * P], ident[:])
-        for u in range(HALVES):
+        for u in range(TURNED):
             for h in range(HALVES):
                 activate(results[h][:, u * P : (u + 1) * P], banks[u][:, h * P : (h + 1) * P], h)
         for h in range(HALVES):
             store(h)
 
-        matmuls(2, v_back, S // 2, S)
+        scales_back = placed(turned_ts, "scales_back", [P, M // 4], I32, 0)
+        nc.gpsimd.tensor_copy(out=scales_back[:], in_=w_scales[2].bitcast(I32))
+        for h in range(HALVES):
+            w_scales[2, h] = scales_back[:].bitcast(U8)[:, h * P : (h + 1) * P]
+
+        matmuls(2, v_back, S // 2, S // 2, S - TOKENS)
+        for h in range(HALVES):
+            matmuls(2, v_back, S // 2, S - TOKENS, S, [h], closing=1)
+            matmuls(1, v_codes1, 0, S - TOKENS, S, [h], closing=1)
         for i in range(HALVES, len(SUMS)):
             h, lo = SUMS[i]
             scaled = sbuf(f"scaled{i}", [P, TOKENS], F32)

@@ -143,9 +143,9 @@ def tile_list_tabts_silu_kernel(tc, tab_words, tab_scales, w, ts, b, offs, out):
                 out=ts_cols[:, per_bank * i : per_bank * (i + 1)],
                 in_=bank[:].rearrange("p (u c) -> p u c", c=P)[:, :, TS_ROW],
             )
-        ts_turned = [placed(turned_ts, "ts_turned0", [P, 1], F32, 0), sbuf("ts_turned1", [P, 1], F32)]
+        ts_turned = [placed(turned_ts, "ts_turned0", [P, M // 4 + HALVES * TOKENS], F32, 0), sbuf("ts_turned1", [P, 1], F32)]
         for u in range(TURNED):
-            nc.scalar.copy(out=ts_turned[u][:], in_=turned[0][:, u * P + TS_ROW : u * P + TS_ROW + 1])
+            nc.scalar.copy(out=ts_turned[u][:, 0:1], in_=turned[0][:, u * P + TS_ROW : u * P + TS_ROW + 1])
         round_w(w_early[:, M : 2 * M, :], w_raw[1][:])
         for u in range(blocks - TURNED):
             place = slice(u % per_bank * P, (u % per_bank + 1) * P)
@@ -190,7 +190,7 @@ def tile_list_tabts_silu_kernel(tc, tab_words, tab_scales, w, ts, b, offs, out):
 
         v_codes1 = placed(late, "v_codes1", [P, S], U32, 2 * WORD_BYTES + RAW_BYTES)
         gather(v_codes1, windows[1][:].bitcast(U32))
-        matmuls(1, v_codes1, 0, 0, S - TOKENS)
+        matmuls(1, v_codes1, 0, 0, S)
 
         window2 = windows[2][:].bitcast(U32)
         w_late = sbuf("w_late", [P, M, PACK], BF16)
@@ -225,7 +225,7 @@ def tile_list_tabts_silu_kernel(tc, tab_words, tab_scales, w, ts, b, offs, out):
         ]
         for u in range(TURNED):
             nc.scalar.activation(
-                out=by_token[u][:, 0:M], in_=banks[u][:, 0:M], func=ACT.Copy, scale=ts_turned[u][:]
+                out=by_token[u][:, 0:M], in_=banks[u][:, 0:M], func=ACT.Copy, scale=ts_turned[u][:, 0:1]
             )
         for u in range(TURNED):
             for h in range(HALVES):
@@ -237,17 +237,17 @@ def tile_list_tabts_silu_kernel(tc, tab_words, tab_scales, w, ts, b, offs, out):
             store(h)
 
         scales_back = placed(turned_ts, "scales_back", [P, M // 4], I32, 0)
-        nc.gpsimd.tensor_copy(out=scales_back[:], in_=w_scales[2].bitcast(I32))
+        nc.vector.tensor_copy(out=scales_back[:], in_=w_scales[2].bitcast(I32))
         for h in range(HALVES):
             w_scales[2, h] = scales_back[:].bitcast(U8)[:, h * P : (h + 1) * P]
 
-        matmuls(2, v_back, S // 2, S // 2, S - TOKENS)
-        for h in range(HALVES):
-            matmuls(2, v_back, S // 2, S - TOKENS, S, [h], closing=1)
-            matmuls(1, v_codes1, 0, S - TOKENS, S, [h], closing=1)
+        matmuls(2, v_back, S // 2, S // 2, S)
         for i in range(HALVES, len(SUMS)):
             h, lo = SUMS[i]
-            scaled = sbuf(f"scaled{i}", [P, TOKENS], F32)
+            if i < 2 * HALVES:
+                scaled = placed(turned_ts, f"scaled{i}", [P, TOKENS], F32, M + 4 * TOKENS * h)
+            else:
+                scaled = sbuf(f"scaled{i}", [P, TOKENS], F32)
             nc.vector.tensor_tensor(
                 out=scaled[:], in0=banks[i][:, 0:TOKENS], in1=ts_rows[:, lo - TOKENS : lo], op=ALU.mult
             )

@@ -27,6 +27,7 @@ TS_ROW = P - 1
 RAW_BYTES = PACK * M * 4
 WORD_BYTES = 4 * T
 TOKENS = 256
+SHARED = (TOKENS, 2 * TOKENS)
 TURNED = TOKENS // P
 SUMS = [(h, lo) for lo in range(0, S, TOKENS) for h in range(HALVES)]
 
@@ -133,7 +134,7 @@ def tile_list_tabts_silu_kernel(tc, tab_words, tab_scales, w, ts, b, offs, out):
 
         blocks = S // P
         per_bank = BANK // P
-        turned, spread = banks[6:8], banks[4:6]
+        turned, spread = banks[6:8], banks[2:4]
         ts_cols = placed(first_weights, "ts_cols", [P, RAW_BYTES // 4], F32, 0)
         for u in range(blocks):
             place = slice(u % per_bank * P, (u % per_bank + 1) * P)
@@ -143,7 +144,7 @@ def tile_list_tabts_silu_kernel(tc, tab_words, tab_scales, w, ts, b, offs, out):
                 out=ts_cols[:, per_bank * i : per_bank * (i + 1)],
                 in_=bank[:].rearrange("p (u c) -> p u c", c=P)[:, :, TS_ROW],
             )
-        ts_turned = [placed(turned_ts, "ts_turned0", [P, M // 4 + HALVES * TOKENS], F32, 0), sbuf("ts_turned1", [P, 1], F32)]
+        ts_turned = [placed(turned_ts, "ts_turned0", [P, M // 4 + (1 + HALVES) * TOKENS], F32, 0), sbuf("ts_turned1", [P, 1], F32)]
         for u in range(TURNED):
             nc.scalar.copy(out=ts_turned[u][:, 0:1], in_=turned[0][:, u * P + TS_ROW : u * P + TS_ROW + 1])
         round_w(w_early[:, M : 2 * M, :], w_raw[1][:])
@@ -156,8 +157,13 @@ def tile_list_tabts_silu_kernel(tc, tab_words, tab_scales, w, ts, b, offs, out):
             width = min(BANK, S - TOKENS - i * BANK)
             nc.scalar.copy(out=ts_rows[:, i * BANK : i * BANK + width], in_=bank[:, 0:width])
 
+        places = [(banks[0], 0), (banks[1], 0), (banks[4], 0), (banks[4], TOKENS)]
+        places = places + [(banks[5], 0), (banks[5], TOKENS), (banks[6], 0), (banks[7], 0)]
+        spare = banks[2:4]
+
         def matmuls(a, v_codes, first, lo_sum, hi_sum, halves=range(HALVES), closing=PASSES - 1):
-            for bank, (h, lo) in zip(banks, SUMS):
+            for (bank, column), (h, lo) in zip(places, SUMS):
+                shared = lo in SHARED
                 if not (lo_sum <= lo < hi_sum and h in halves):
                     continue
                 if lo == 0:
@@ -170,11 +176,11 @@ def tile_list_tabts_silu_kernel(tc, tab_words, tab_scales, w, ts, b, offs, out):
                     )
                     continue
                 nc.tensor.matmul_mx(
-                    out=bank[:, 0:TOKENS],
+                    out=bank[:, column : column + TOKENS],
                     lhsT=w_codes[a, h].bitcast(FP8X4), lhsT_scale=w_scales[a, h],
                     rhs=v_codes[:, lo - first : lo - first + TOKENS].bitcast(FP8X4),
                     rhs_scale=v_scales[4 * a : P, lo : lo + TOKENS],
-                    start=(a == 0), stop=(a == closing),
+                    start=(a == 0 and column == 0), stop=(a == closing and (h == HALVES - 1 or not shared)),
                 )
 
         v_codes0 = sbuf("v_codes0", [P, S], U32)
@@ -190,7 +196,7 @@ def tile_list_tabts_silu_kernel(tc, tab_words, tab_scales, w, ts, b, offs, out):
 
         v_codes1 = placed(late, "v_codes1", [P, S], U32, 2 * WORD_BYTES + RAW_BYTES)
         gather(v_codes1, windows[1][:].bitcast(U32))
-        matmuls(1, v_codes1, 0, 0, S)
+        matmuls(1, v_codes1, 0, 0, S - TOKENS)
 
         window2 = windows[2][:].bitcast(U32)
         w_late = sbuf("w_late", [P, M, PACK], BF16)
@@ -203,8 +209,8 @@ def tile_list_tabts_silu_kernel(tc, tab_words, tab_scales, w, ts, b, offs, out):
             v_front = placed(late, f"v_front{lo}", [P, TOKENS], U32, raw2 + 4 * lo)
             gather(v_front, window2, lo, lo + TOKENS)
             matmuls(2, v_front, lo, lo, lo + TOKENS)
-        v_back = placed(late, "v_back", [P, S // 2], U32, raw2 + 2 * S)
-        gather(v_back, window2, S // 2, S)
+        v_third = placed(late, "v_third", [P, TOKENS], U32, raw2 + 2 * S)
+        gather(v_third, window2, S // 2, S - TOKENS)
 
         results = [sbuf(f"result{i}", [P, TOKENS], F32) for i in range(HALVES)]
         results = results + [
@@ -223,16 +229,19 @@ def tile_list_tabts_silu_kernel(tc, tab_words, tab_scales, w, ts, b, offs, out):
             sbuf("by_token0", [P, M], F32),
             placed(last_turned, "by_token1", [P, TOKENS * (len(SUMS) - HALVES)], F32, 0),
         ]
-        for u in range(TURNED):
-            nc.scalar.activation(
-                out=by_token[u][:, 0:M], in_=banks[u][:, 0:M], func=ACT.Copy, scale=ts_turned[u][:, 0:1]
-            )
+        back = {(u, h): (spare[u] if h == 0 else banks[u])[:, 0:P] for u in range(TURNED) for h in range(HALVES)}
         for u in range(TURNED):
             for h in range(HALVES):
-                nc.tensor.transpose(banks[u][:, h * P : (h + 1) * P], by_token[u][:, h * P : (h + 1) * P], ident[:])
+                nc.scalar.activation(
+                    out=by_token[u][:, h * P : (h + 1) * P], in_=banks[u][:, h * P : (h + 1) * P],
+                    func=ACT.Copy, scale=ts_turned[u][:, 0:1],
+                )
         for u in range(TURNED):
             for h in range(HALVES):
-                activate(results[h][:, u * P : (u + 1) * P], banks[u][:, h * P : (h + 1) * P], h)
+                nc.tensor.transpose(back[u, h], by_token[u][:, h * P : (h + 1) * P], ident[:])
+        for u in range(TURNED):
+            for h in range(HALVES):
+                activate(results[h][:, u * P : (u + 1) * P], back[u, h], h)
         for h in range(HALVES):
             store(h)
 
@@ -241,15 +250,20 @@ def tile_list_tabts_silu_kernel(tc, tab_words, tab_scales, w, ts, b, offs, out):
         for h in range(HALVES):
             w_scales[2, h] = scales_back[:].bitcast(U8)[:, h * P : (h + 1) * P]
 
-        matmuls(2, v_back, S // 2, S // 2, S)
+        matmuls(2, v_third, S // 2, S // 2, S - TOKENS)
+        v_last = placed(turned_ts, "v_last", [P, TOKENS], U32, M)
+        gather(v_last, window2, S - TOKENS, S)
+        for h in range(HALVES):
+            matmuls(2, v_last, S - TOKENS, S - TOKENS, S, [h], closing=1)
+            matmuls(1, v_codes1, 0, S - TOKENS, S, [h], closing=1)
         for i in range(HALVES, len(SUMS)):
             h, lo = SUMS[i]
             if i < 2 * HALVES:
-                scaled = placed(turned_ts, f"scaled{i}", [P, TOKENS], F32, M + 4 * TOKENS * h)
+                scaled = placed(turned_ts, f"scaled{i}", [P, TOKENS], F32, M + 4 * TOKENS * (1 + h))
             else:
                 scaled = sbuf(f"scaled{i}", [P, TOKENS], F32)
             nc.vector.tensor_tensor(
-                out=scaled[:], in0=banks[i][:, 0:TOKENS], in1=ts_rows[:, lo - TOKENS : lo], op=ALU.mult
+                out=scaled[:], in0=places[i][0][:, places[i][1] : places[i][1] + TOKENS], in1=ts_rows[:, lo - TOKENS : lo], op=ALU.mult
             )
             activate(results[i][:], scaled[:], h)
             store(i)

@@ -20,16 +20,17 @@ P = 128
 PACK = 4
 K_PASS = P * PACK
 PASSES = K // K_PASS
-QUADRANTS = 4
+QUADRANTS = (0, 1, 2, 3)
 BANK = 512
 HALVES = M // P
 TS_ROW = P - 1
 RAW_BYTES = PACK * M * 4
 WORD_BYTES = 4 * T
-TOKENS = 256
-SHARED = (TOKENS, 2 * TOKENS)
-TURNED = TOKENS // P
-SUMS = [(h, lo) for lo in range(0, S, TOKENS) for h in range(HALVES)]
+TURNED = 3
+FRONT = TURNED * P
+SCALE_CUT = FRONT + P
+STRAIGHT = [(FRONT, P, ((3, 0), (3, P))), (FRONT + P, 384, ((4, 0), (5, 0))), (S - P, P, ((6, 0), (7, 0)))]
+WIDE = 256
 
 
 def tile_list_tabts_silu_kernel(tc, tab_words, tab_scales, w, ts, b, offs, out):
@@ -41,7 +42,7 @@ def tile_list_tabts_silu_kernel(tc, tab_words, tab_scales, w, ts, b, offs, out):
         first_weights = ctx.enter_context(tc.tile_pool(name="first_weights", bufs=1))
         picked_ts = ctx.enter_context(tc.tile_pool(name="picked_ts", bufs=1))
         early_rounded = ctx.enter_context(tc.tile_pool(name="early_rounded", bufs=1))
-        turned_ts = ctx.enter_context(tc.tile_pool(name="turned_ts", bufs=1))
+        first_ts = ctx.enter_context(tc.tile_pool(name="first_ts", bufs=1))
         last_turned = ctx.enter_context(tc.tile_pool(name="last_turned", bufs=1))
         psum = ctx.enter_context(tc.psum_pool(name="psum", bufs=1))
 
@@ -56,14 +57,14 @@ def tile_list_tabts_silu_kernel(tc, tab_words, tab_scales, w, ts, b, offs, out):
         scale_window = sbuf("scale_window", [P, T // 4], I32)
         ts_picked = placed(picked_ts, "ts_picked", [P, S], F32, 0)
         ident = sbuf("ident", [P, P], F32)
-        banks = [psum.tile([P, BANK], F32, name=f"bank{i}") for i in range(len(SUMS))]
+        banks = [psum.tile([P, BANK], F32, name=f"bank{i}") for i in range(8)]
 
         def load_words(a, window):
             nc.sync.dma_start(out=window[:], in_=tab_words[a].rearrange("p t i -> p (t i)").bitcast(I32))
 
-        def load_w(a, raw, lo=0, hi=PACK):
+        def load_w(a, raw):
             rows = w[K_PASS * a : K_PASS * (a + 1), :]
-            nc.sync.dma_start(out=raw[:], in_=rows.rearrange("(p i) n -> p i n", i=PACK)[:, lo:hi, :])
+            nc.sync.dma_start(out=raw[:], in_=rows.rearrange("(p i) n -> p i n", i=PACK))
 
         nc.sync.dma_start(offsets[:], offs)
         nc.scalar.dma_start(out=ts_window[TS_ROW:P, :], in_=ts[0:1, :])
@@ -77,6 +78,8 @@ def tile_list_tabts_silu_kernel(tc, tab_words, tab_scales, w, ts, b, offs, out):
             fill=1.0, base=0, pattern=[[-1, P]], channel_multiplier=1,
         )
 
+        raw1 = 2 * WORD_BYTES + RAW_BYTES // 2
+        raw2 = 2 * WORD_BYTES + 2 * RAW_BYTES
         windows = [
             placed(first_words, "word_window0", [P, T], I32, 0),
             placed(late, "word_window1", [P, T], I32, 0),
@@ -84,15 +87,14 @@ def tile_list_tabts_silu_kernel(tc, tab_words, tab_scales, w, ts, b, offs, out):
         ]
         w_raw = [
             placed(first_weights, "w_raw0", [P, PACK, M], F32, 0),
-            placed(late, "w_raw1", [P, PACK, M], F32, 2 * WORD_BYTES + RAW_BYTES // 2),
+            placed(late, "w_raw1", [P, PACK, M], F32, raw1),
+            placed(late, "w_raw2", [P, PACK, M], F32, raw2),
         ]
-        raw2 = 2 * WORD_BYTES + 2 * RAW_BYTES
-        w_raw.append(placed(late, "w_raw2", [P, PACK, M], F32, raw2))
-        bias = placed(late, "bias", [P, HALVES], F32, 2 * WORD_BYTES + 3 * RAW_BYTES)
+        bias = placed(late, "bias", [P, HALVES], F32, raw2 + RAW_BYTES)
 
         load_words(0, windows[0])
         load_w(0, w_raw[0])
-        for q in range(QUADRANTS):
+        for q in QUADRANTS:
             nc.sync.dma_start(
                 out=scale_window[32 * q : 32 * q + 4 * PASSES, :],
                 in_=tab_scales[:, 4 * q : 4 * q + 4, :].bitcast(I32),
@@ -107,163 +109,159 @@ def tile_list_tabts_silu_kernel(tc, tab_words, tab_scales, w, ts, b, offs, out):
         def gather(picked, window, lo=0, hi=S):
             nc.vector.tensor_copy(out=picked[:], in_=window.indirect(offsets[:, lo // 16 : hi // 16]))
 
-        w_codes, w_scales = {}, {}
-
         def round_w(rounded, raw):
             nc.scalar.copy(
                 out=rounded.rearrange("p (c j) i -> p c i j", j=4),
                 in_=raw.rearrange("p i (c j) -> p c i j", j=4),
             )
 
-        def quantize_w(rounded, groups, codes, scales):
+        def quantize_w(rounded, codes, scales):
             nc.vector.quantize_mx(
-                out=codes[:].bitcast(FP8X4), scales=scales[:], in_=rounded.rearrange("p n i -> p (n i)")
+                out=codes[:].bitcast(FP8X4), scales=scales, in_=rounded.rearrange("p n i -> p (n i)")
             )
-            for j, group in enumerate(groups):
-                w_codes[group] = codes[:, j * P : (j + 1) * P]
-                w_scales[group] = scales[:, j * P : (j + 1) * P]
-                if group[1] == 0:
-                    w_codes[group[0]] = codes[:, j * P : j * P + M]
-                    w_scales[group[0]] = scales[:, j * P : j * P + M]
 
         gather(ts_picked, ts_window[:])
-        w_early = placed(early_rounded, "w_early", [P, 2 * M, PACK], BF16, 0)
+        w_early = [sbuf("w_early0", [P, M, PACK], BF16), placed(early_rounded, "w_early1", [P, M, PACK], BF16, 0)]
         warm = sbuf("warm", [P, 1], F32)
         nc.scalar.activation(out=warm[:], in_=w_raw[0][:, 0, 0:1], func=ACT.Silu)
-        round_w(w_early[:, 0:M, :], w_raw[0][:])
+        round_w(w_early[0][:], w_raw[0][:])
 
         blocks = S // P
         per_bank = BANK // P
-        turned, spread = banks[6:8], banks[2:4]
-        ts_cols = placed(first_weights, "ts_cols", [P, RAW_BYTES // 4], F32, 0)
+        ts_banks = banks[6:8]
+        ts_cols = placed(first_weights, "ts_cols", [P, blocks], F32, 0)
+        ts_first = placed(first_ts, "ts_first", [P, M // 4], F32, 0)
+        ts_front = sbuf("ts_front", [P, TURNED], F32)
         for u in range(blocks):
             place = slice(u % per_bank * P, (u % per_bank + 1) * P)
-            nc.tensor.transpose(turned[u // per_bank][:, place], ts_picked[:, u * P : (u + 1) * P], ident[:])
-        for i, bank in enumerate(turned):
+            nc.tensor.transpose(ts_banks[u // per_bank][:, place], ts_picked[:, u * P : (u + 1) * P], ident[:])
+        for i, bank in enumerate(ts_banks):
             nc.scalar.copy(
                 out=ts_cols[:, per_bank * i : per_bank * (i + 1)],
                 in_=bank[:].rearrange("p (u c) -> p u c", c=P)[:, :, TS_ROW],
             )
-        ts_turned = [placed(turned_ts, "ts_turned0", [P, M // 4 + (1 + HALVES) * TOKENS], F32, 0), sbuf("ts_turned1", [P, 1], F32)]
-        for u in range(TURNED):
-            nc.scalar.copy(out=ts_turned[u][:, 0:1], in_=turned[0][:, u * P + TS_ROW : u * P + TS_ROW + 1])
-        round_w(w_early[:, M : 2 * M, :], w_raw[1][:])
+        nc.scalar.copy(out=ts_first[:, 0:1], in_=ts_banks[0][:, P + TS_ROW : 2 * P])
+        nc.scalar.copy(out=ts_front[:], in_=ts_banks[0][:].rearrange("p (u c) -> p u c", c=P)[:, 0:TURNED, TS_ROW])
+        round_w(w_early[1][:], w_raw[1][:])
         for u in range(blocks - TURNED):
             place = slice(u % per_bank * P, (u % per_bank + 1) * P)
             column = ts_cols[:, TURNED + u : TURNED + u + 1]
-            nc.tensor.transpose(spread[u // per_bank][:, place], column.to_broadcast([P, P]), ident[:])
-        ts_rows = placed(late, "ts_rows", [P, S - TOKENS], F32, 2 * WORD_BYTES)
-        for i, bank in enumerate(spread):
-            width = min(BANK, S - TOKENS - i * BANK)
+            nc.tensor.transpose(ts_banks[u // per_bank][:, place], column.to_broadcast([P, P]), ident[:])
+        ts_rows = placed(late, "ts_rows", [P, S - FRONT], F32, 2 * WORD_BYTES)
+        for i, bank in enumerate(ts_banks):
+            width = min(BANK, S - FRONT - i * BANK)
             nc.scalar.copy(out=ts_rows[:, i * BANK : i * BANK + width], in_=bank[:, 0:width])
 
-        places = [(banks[0], 0), (banks[1], 0), (banks[4], 0), (banks[4], TOKENS)]
-        places = places + [(banks[5], 0), (banks[5], TOKENS), (banks[6], 0), (banks[7], 0)]
-        spare = banks[2:4]
+        def turned_pass(a, u, v_codes, w_codes, w_scales):
+            nc.tensor.matmul_mx(
+                out=banks[u][:, 0:M],
+                lhsT=v_codes.bitcast(FP8X4), lhsT_scale=part_of(scale_parts, SCALE_CUT, u * P, P)[4 * a : P, :],
+                rhs=w_codes.bitcast(FP8X4), rhs_scale=w_scales,
+                start=(a == 0), stop=(a == PASSES - 1),
+            )
 
-        def matmuls(a, v_codes, first, lo_sum, hi_sum, halves=range(HALVES), closing=PASSES - 1):
-            for (bank, column), (h, lo) in zip(places, SUMS):
-                shared = lo in SHARED
-                if not (lo_sum <= lo < hi_sum and h in halves):
-                    continue
-                if lo == 0:
+        def straight_pass(a, entry, v_codes, w_codes, w_scales):
+            lo, tokens, places = entry
+            shared = places[0][0] == places[1][0]
+            for h, (bank, column) in enumerate(places):
+                for at in range(0, tokens, WIDE):
+                    end = min(at + WIDE, tokens)
                     nc.tensor.matmul_mx(
-                        out=bank[:, 0:M],
-                        lhsT=v_codes[:, h * P : (h + 1) * P].bitcast(FP8X4),
-                        lhsT_scale=v_scales[4 * a : P, h * P : (h + 1) * P],
-                        rhs=w_codes[a].bitcast(FP8X4), rhs_scale=w_scales[a],
-                        start=(a == 0), stop=(a == PASSES - 1),
+                        out=banks[bank][:, column + at : column + end],
+                        lhsT=w_codes[:, h * P : (h + 1) * P].bitcast(FP8X4), lhsT_scale=w_scales[:, h * P : (h + 1) * P],
+                        rhs=v_codes[:, at:end].bitcast(FP8X4), rhs_scale=part_of(scale_parts, SCALE_CUT, lo + at, end - at)[4 * a : P, :],
+                        start=(a == 0 and column + at == 0),
+                        stop=(a == PASSES - 1 and end == tokens and (h == HALVES - 1 or not shared)),
                     )
-                    continue
-                nc.tensor.matmul_mx(
-                    out=bank[:, column : column + TOKENS],
-                    lhsT=w_codes[a, h].bitcast(FP8X4), lhsT_scale=w_scales[a, h],
-                    rhs=v_codes[:, lo - first : lo - first + TOKENS].bitcast(FP8X4),
-                    rhs_scale=v_scales[4 * a : P, lo : lo + TOKENS],
-                    start=(a == 0 and column == 0), stop=(a == closing and (h == HALVES - 1 or not shared)),
-                )
+
+        def whole_pass(a, codes_of, w_codes, w_scales):
+            for u in range(TURNED):
+                turned_pass(a, u, codes_of(u * P, P), w_codes, w_scales)
+            for entry in STRAIGHT:
+                straight_pass(a, entry, codes_of(entry[0], entry[1]), w_codes, w_scales)
+
+        def part_of(parts, cut, lo, n):
+            return parts[0][:, lo : lo + n] if lo < cut else parts[1][:, lo - cut : lo - cut + n]
 
         v_codes0 = sbuf("v_codes0", [P, S], U32)
         gather(v_codes0, windows[0][:].bitcast(U32))
-        v_scales = placed(picked_ts, "v_scales", [P, S], U8, 0)
-        gather(v_scales, scale_window[:].bitcast(U8))
-        quantize_w(
-            w_early[:], [(a, h) for a in range(2) for h in range(HALVES)],
-            placed(first_words, "w_codes_early", [P, 2 * M], U32, S),
-            placed(first_weights, "w_scales_early", [P, 2 * M], U8, 0),
-        )
-        matmuls(0, v_codes0, 0, 0, S)
+        scale_parts = [placed(picked_ts, "v_scales0", [P, SCALE_CUT], U8, 0), placed(first_weights, "v_scales1", [P, S - SCALE_CUT], U8, 1024)]
+        gather(scale_parts[0], scale_window[:].bitcast(U8), 0, SCALE_CUT)
+        w_codes = [sbuf(f"w_codes{a}", [P, M], U32) for a in range(2)]
+        w_scales = [sbuf(f"w_scales{a}", [P, M], U8) for a in range(2)]
+        quantize_w(w_early[0][:], w_codes[0], w_scales[0][:])
+        gather(scale_parts[1], scale_window[:].bitcast(U8), SCALE_CUT, S)
+        whole_pass(0, lambda lo, n: v_codes0[:, lo : lo + n], w_codes[0][:], w_scales[0][:])
 
-        v_codes1 = placed(late, "v_codes1", [P, S], U32, 2 * WORD_BYTES + RAW_BYTES)
-        gather(v_codes1, windows[1][:].bitcast(U32))
-        matmuls(1, v_codes1, 0, 0, S - TOKENS)
+        quantize_w(w_early[1][:], w_codes[1], w_scales[1][:])
+        at = 2 * WORD_BYTES + 4 * (S - FRONT)
+        parts = [placed(late, "v_codes1a", [P, FRONT], U32, at), placed(late, "v_codes1b", [P, S - FRONT], U32, at + 4 * FRONT)]
+        gather(parts[0], windows[1][:].bitcast(U32), 0, FRONT)
+        gather(parts[1], windows[1][:].bitcast(U32), FRONT, S)
+        whole_pass(1, lambda lo, n: part_of(parts, FRONT, lo, n), w_codes[1][:], w_scales[1][:])
 
         window2 = windows[2][:].bitcast(U32)
         w_late = sbuf("w_late", [P, M, PACK], BF16)
         round_w(w_late[:], w_raw[2][:])
-        quantize_w(
-            w_late[:], [(2, h) for h in range(HALVES)],
-            placed(early_rounded, "w_codes2", [P, M], U32, 0), sbuf("w_scales2", [P, M], U8),
+        codes_late = placed(early_rounded, "w_codes2", [P, M], U32, 0)
+        scales_late = sbuf("w_scales_late", [P, M], U8)
+        quantize_w(w_late[:], codes_late, scales_late[:])
+        for u in range(TURNED):
+            v_block = placed(late, f"v_block{u}", [P, P], U32, raw2 + 4 * P * u)
+            gather(v_block, window2, u * P, (u + 1) * P)
+            turned_pass(2, u, v_block[:], codes_late[:], scales_late[:])
+        v_straight = []
+        for lo, tokens, places in STRAIGHT:
+            v_straight.append(placed(late, f"v_straight{lo}", [P, tokens], U32, raw2 + 4 * lo))
+            gather(v_straight[-1], window2, lo, lo + tokens)
+        straight_pass(2, STRAIGHT[0], v_straight[0][:], codes_late[:], scales_late[:])
+
+        by_token = [sbuf(f"by_token{u}", [P, M], F32) for u in range(TURNED - 1)]
+        by_token.append(placed(last_turned, "by_token2", [P, M], F32, 2 * M))
+        outer = [sbuf(f"result{h}", [P, S], F32) for h in range(HALVES)]
+        inner = [placed(last_turned, f"inner{h}", [P, 2 * P], F32, 4 * M * h) for h in range(HALVES)]
+
+        def result(h, lo, hi):
+            return inner[h][:, lo - 2 * P : hi - 2 * P] if 2 * P <= lo < 4 * P else outer[h][:, lo:hi]
+
+        def activate(h, lo, tokens, scaled):
+            nc.scalar.activation(out=result(h, lo, lo + tokens), in_=scaled, func=ACT.Silu, bias=bias[:, h : h + 1])
+
+        def store(h, lo, hi):
+            nc.sync.dma_start(out=out[h * P : (h + 1) * P, lo:hi], in_=result(h, lo, hi))
+
+        for u in range(TURNED):
+            scale = ts_first[:, 0:1] if u == 1 else ts_front[:, u : u + 1]
+            nc.scalar.activation(out=by_token[u][:], in_=banks[u][:, 0:M], func=ACT.Copy, scale=scale)
+        scales_moved = placed(first_ts, "scales_moved", [P, M // 4], U32, 0)
+        nc.scalar.copy(out=scales_moved[:], in_=scales_late[:].bitcast(U32))
+        for h in range(HALVES):
+            for u in range(2):
+                nc.tensor.transpose(banks[h][:, u * P : (u + 1) * P], by_token[u][:, h * P : (h + 1) * P], ident[:])
+        for h in range(HALVES):
+            nc.tensor.transpose(banks[2][:, h * P : (h + 1) * P], by_token[2][:, h * P : (h + 1) * P], ident[:])
+        for h in range(HALVES):
+            activate(h, 0, 2 * P, banks[h][:, 0 : 2 * P])
+            store(h, 0, 2 * P)
+        for h in range(HALVES):
+            activate(h, 2 * P, P, banks[2][:, h * P : (h + 1) * P])
+
+        for entry, v_codes in zip(STRAIGHT[1:], v_straight[1:]):
+            straight_pass(2, entry, v_codes[:], codes_late[:], scales_moved[:].bitcast(U8))
+        both = sbuf("scaled_both", [P, HALVES, P], F32)
+        nc.vector.tensor_tensor(
+            out=both[:], in0=banks[3][:, 0:M].rearrange("p (h t) -> p h t", h=HALVES),
+            in1=ts_rows[:, 0:P].unsqueeze(1).to_broadcast([P, HALVES, P]), op=ALU.mult,
         )
-        for lo in (0, TOKENS):
-            v_front = placed(late, f"v_front{lo}", [P, TOKENS], U32, raw2 + 4 * lo)
-            gather(v_front, window2, lo, lo + TOKENS)
-            matmuls(2, v_front, lo, lo, lo + TOKENS)
-        v_third = placed(late, "v_third", [P, TOKENS], U32, raw2 + 2 * S)
-        gather(v_third, window2, S // 2, S - TOKENS)
-
-        results = [sbuf(f"result{i}", [P, TOKENS], F32) for i in range(HALVES)]
-        results = results + [
-            placed(last_turned, f"result{i}", [P, TOKENS], F32, 4 * TOKENS * (i - HALVES))
-            for i in range(HALVES, len(SUMS))
-        ]
-
-        def store(i):
-            h, lo = SUMS[i]
-            nc.sync.dma_start(out=out[h * P : (h + 1) * P, lo : lo + TOKENS], in_=results[i][:])
-
-        def activate(result, scaled, h):
-            nc.scalar.activation(out=result, in_=scaled, func=ACT.Silu, bias=bias[:, h : h + 1])
-
-        by_token = [
-            sbuf("by_token0", [P, M], F32),
-            placed(last_turned, "by_token1", [P, TOKENS * (len(SUMS) - HALVES)], F32, 0),
-        ]
-        back = {(u, h): (spare[u] if h == 0 else banks[u])[:, 0:P] for u in range(TURNED) for h in range(HALVES)}
-        for u in range(TURNED):
-            for h in range(HALVES):
-                nc.scalar.activation(
-                    out=by_token[u][:, h * P : (h + 1) * P], in_=banks[u][:, h * P : (h + 1) * P],
-                    func=ACT.Copy, scale=ts_turned[u][:, 0:1],
+        for h in range(HALVES):
+            activate(h, FRONT, P, both[:, h, :])
+            store(h, 2 * P, 4 * P)
+        for lo, tokens, places in STRAIGHT[1:]:
+            for h, (bank, column) in enumerate(places):
+                scaled = sbuf(f"scaled{lo}_{h}", [P, tokens], F32)
+                nc.vector.tensor_tensor(
+                    out=scaled[:], in0=banks[bank][:, 0:tokens],
+                    in1=ts_rows[:, lo - FRONT : lo - FRONT + tokens], op=ALU.mult,
                 )
-        for u in range(TURNED):
-            for h in range(HALVES):
-                nc.tensor.transpose(back[u, h], by_token[u][:, h * P : (h + 1) * P], ident[:])
-        for u in range(TURNED):
-            for h in range(HALVES):
-                activate(results[h][:, u * P : (u + 1) * P], back[u, h], h)
-        for h in range(HALVES):
-            store(h)
-
-        scales_back = placed(turned_ts, "scales_back", [P, M // 4], I32, 0)
-        nc.vector.tensor_copy(out=scales_back[:], in_=w_scales[2].bitcast(I32))
-        for h in range(HALVES):
-            w_scales[2, h] = scales_back[:].bitcast(U8)[:, h * P : (h + 1) * P]
-
-        matmuls(2, v_third, S // 2, S // 2, S - TOKENS)
-        v_last = placed(turned_ts, "v_last", [P, TOKENS], U32, M)
-        gather(v_last, window2, S - TOKENS, S)
-        for h in range(HALVES):
-            matmuls(2, v_last, S - TOKENS, S - TOKENS, S, [h], closing=1)
-            matmuls(1, v_codes1, 0, S - TOKENS, S, [h], closing=1)
-        for i in range(HALVES, len(SUMS)):
-            h, lo = SUMS[i]
-            if i < 2 * HALVES:
-                scaled = placed(turned_ts, f"scaled{i}", [P, TOKENS], F32, M + 4 * TOKENS * (1 + h))
-            else:
-                scaled = sbuf(f"scaled{i}", [P, TOKENS], F32)
-            nc.vector.tensor_tensor(
-                out=scaled[:], in0=places[i][0][:, places[i][1] : places[i][1] + TOKENS], in1=ts_rows[:, lo - TOKENS : lo], op=ALU.mult
-            )
-            activate(results[i][:], scaled[:], h)
-            store(i)
+                activate(h, lo, tokens, scaled[:])
+                store(h, lo, lo + tokens)

@@ -26,10 +26,10 @@ HALVES = M // P
 TS_ROW = P - 1
 RAW_BYTES = PACK * M * 4
 WORD_BYTES = 4 * T
-TURNED = 3
+TURNED = 2
 FRONT = TURNED * P
-SCALE_CUT = FRONT + P
-STRAIGHT = [(FRONT, P, ((3, 0), (3, P))), (FRONT + P, 384, ((4, 0), (5, 0))), (S - P, P, ((6, 0), (7, 0)))]
+SCALE_CUT = S // 2
+STRAIGHT = [(FRONT, 256, ((2, 0), (3, 0))), (FRONT + 256, 256, ((4, 0), (4, 256))), (S - 256, 256, ((5, 0), (6, 0)))]
 WIDE = 256
 
 
@@ -140,7 +140,7 @@ def tile_list_tabts_silu_kernel(tc, tab_words, tab_scales, w, ts, b, offs, out):
                 out=ts_cols[:, per_bank * i : per_bank * (i + 1)],
                 in_=bank[:].rearrange("p (u c) -> p u c", c=P)[:, :, TS_ROW],
             )
-        nc.scalar.copy(out=ts_first[:, 0:1], in_=ts_banks[0][:, P + TS_ROW : 2 * P])
+        nc.scalar.copy(out=ts_first[:, 0:1], in_=ts_banks[0][:, TS_ROW:P])
         nc.scalar.copy(out=ts_front[:], in_=ts_banks[0][:].rearrange("p (u c) -> p u c", c=P)[:, 0:TURNED, TS_ROW])
         round_w(w_early[1][:], w_raw[1][:])
         for u in range(blocks - TURNED):
@@ -195,10 +195,10 @@ def tile_list_tabts_silu_kernel(tc, tab_words, tab_scales, w, ts, b, offs, out):
 
         quantize_w(w_early[1][:], w_codes[1], w_scales[1][:])
         at = 2 * WORD_BYTES + 4 * (S - FRONT)
-        parts = [placed(late, "v_codes1a", [P, FRONT], U32, at), placed(late, "v_codes1b", [P, S - FRONT], U32, at + 4 * FRONT)]
-        gather(parts[0], windows[1][:].bitcast(U32), 0, FRONT)
-        gather(parts[1], windows[1][:].bitcast(U32), FRONT, S)
-        whole_pass(1, lambda lo, n: part_of(parts, FRONT, lo, n), w_codes[1][:], w_scales[1][:])
+        parts = [placed(late, "v_codes1a", [P, S // 2], U32, at), placed(late, "v_codes1b", [P, S // 2], U32, at + 2 * S)]
+        gather(parts[0], windows[1][:].bitcast(U32), 0, S // 2)
+        gather(parts[1], windows[1][:].bitcast(U32), S // 2, S)
+        whole_pass(1, lambda lo, n: part_of(parts, S // 2, lo, n), w_codes[1][:], w_scales[1][:])
 
         window2 = windows[2][:].bitcast(U32)
         w_late = sbuf("w_late", [P, M, PACK], BF16)
@@ -216,13 +216,12 @@ def tile_list_tabts_silu_kernel(tc, tab_words, tab_scales, w, ts, b, offs, out):
             gather(v_straight[-1], window2, lo, lo + tokens)
         straight_pass(2, STRAIGHT[0], v_straight[0][:], codes_late[:], scales_late[:])
 
-        by_token = [sbuf(f"by_token{u}", [P, M], F32) for u in range(TURNED - 1)]
-        by_token.append(placed(last_turned, "by_token2", [P, M], F32, 2 * M))
-        outer = [sbuf(f"result{h}", [P, S], F32) for h in range(HALVES)]
-        inner = [placed(last_turned, f"inner{h}", [P, 2 * P], F32, 4 * M * h) for h in range(HALVES)]
+        by_token = [sbuf("by_token0", [P, M], F32), placed(last_turned, "by_token1", [P, S - FRONT + 16], F32, 0)]
+        front = [sbuf(f"front{h}", [P, FRONT], F32) for h in range(HALVES)]
+        rest = [placed(last_turned, f"rest{h}", [P, S - FRONT], F32, 4 * (S - FRONT) * h) for h in range(HALVES)]
 
         def result(h, lo, hi):
-            return inner[h][:, lo - 2 * P : hi - 2 * P] if 2 * P <= lo < 4 * P else outer[h][:, lo:hi]
+            return front[h][:, lo:hi] if lo < FRONT else rest[h][:, lo - FRONT : hi - FRONT]
 
         def activate(h, lo, tokens, scaled):
             nc.scalar.activation(out=result(h, lo, lo + tokens), in_=scaled, func=ACT.Silu, bias=bias[:, h : h + 1])
@@ -231,37 +230,30 @@ def tile_list_tabts_silu_kernel(tc, tab_words, tab_scales, w, ts, b, offs, out):
             nc.sync.dma_start(out=out[h * P : (h + 1) * P, lo:hi], in_=result(h, lo, hi))
 
         for u in range(TURNED):
-            scale = ts_first[:, 0:1] if u == 1 else ts_front[:, u : u + 1]
-            nc.scalar.activation(out=by_token[u][:], in_=banks[u][:, 0:M], func=ACT.Copy, scale=scale)
+            scale = ts_first[:, 0:1] if u == 0 else ts_front[:, u : u + 1]
+            for h in range(HALVES):
+                group = slice(h * P, (h + 1) * P)
+                nc.scalar.activation(out=by_token[u][:, group], in_=banks[u][:, group], func=ACT.Copy, scale=scale)
         scales_moved = placed(first_ts, "scales_moved", [P, M // 4], U32, 0)
         nc.scalar.copy(out=scales_moved[:], in_=scales_late[:].bitcast(U32))
+        back = (banks[7], banks[0])
         for h in range(HALVES):
-            for u in range(2):
-                nc.tensor.transpose(banks[h][:, u * P : (u + 1) * P], by_token[u][:, h * P : (h + 1) * P], ident[:])
+            for u in range(TURNED):
+                nc.tensor.transpose(back[h][:, u * P : (u + 1) * P], by_token[u][:, h * P : (h + 1) * P], ident[:])
         for h in range(HALVES):
-            nc.tensor.transpose(banks[2][:, h * P : (h + 1) * P], by_token[2][:, h * P : (h + 1) * P], ident[:])
-        for h in range(HALVES):
-            activate(h, 0, 2 * P, banks[h][:, 0 : 2 * P])
-            store(h, 0, 2 * P)
-        for h in range(HALVES):
-            activate(h, 2 * P, P, banks[2][:, h * P : (h + 1) * P])
+            activate(h, 0, FRONT, back[h][:, 0:FRONT])
+            store(h, 0, FRONT)
 
         for entry, v_codes in zip(STRAIGHT[1:], v_straight[1:]):
             straight_pass(2, entry, v_codes[:], codes_late[:], scales_moved[:].bitcast(U8))
-        both = sbuf("scaled_both", [P, HALVES, P], F32)
-        nc.vector.tensor_tensor(
-            out=both[:], in0=banks[3][:, 0:M].rearrange("p (h t) -> p h t", h=HALVES),
-            in1=ts_rows[:, 0:P].unsqueeze(1).to_broadcast([P, HALVES, P]), op=ALU.mult,
-        )
-        for h in range(HALVES):
-            activate(h, FRONT, P, both[:, h, :])
-            store(h, 2 * P, 4 * P)
-        for lo, tokens, places in STRAIGHT[1:]:
+        for lo, tokens, places in STRAIGHT:
             for h, (bank, column) in enumerate(places):
-                scaled = sbuf(f"scaled{lo}_{h}", [P, tokens], F32)
-                nc.vector.tensor_tensor(
-                    out=scaled[:], in0=banks[bank][:, 0:tokens],
-                    in1=ts_rows[:, lo - FRONT : lo - FRONT + tokens], op=ALU.mult,
-                )
-                activate(h, lo, tokens, scaled[:])
-                store(h, lo, lo + tokens)
+                width = P if (lo + tokens == S and h == HALVES - 1) else tokens
+                for at in range(0, tokens, width):
+                    scaled = sbuf(f"scaled{lo + at}_{h}", [P, width], F32)
+                    nc.vector.tensor_tensor(
+                        out=scaled[:], in0=banks[bank][:, column + at : column + at + width],
+                        in1=ts_rows[:, lo + at - FRONT : lo + at - FRONT + width], op=ALU.mult,
+                    )
+                    activate(h, lo + at, width, scaled[:])
+                    store(h, lo + at, lo + at + width)

@@ -68,11 +68,11 @@ def tile_list_tabts_silu_kernel(tc, tab_words, tab_scales, w, ts, b, offs, out):
 
         nc.sync.dma_start(offsets[:], offs)
         nc.scalar.dma_start(out=ts_window[TS_ROW:P, :], in_=ts[0:1, :])
-        nc.gpsimd.memset(scale_window[:], 0)
-        nc.vector.memset(ts_window[0:TS_ROW, :], 0.0)
+        nc.vector.memset(scale_window[:], 0)
 
         zeros = placed(late, "zeros", [P, (2 * WORD_BYTES + 3 * RAW_BYTES) // 4 + 16], F32, 0)
-        nc.gpsimd.memset(zeros[:, 0:P], 0.0)
+        nc.vector.memset(zeros[:, 0:P], 0.0)
+        nc.vector.memset(ts_window[0:TS_ROW, :], 0.0)
         nc.gpsimd.affine_select(
             out=ident[:], in_=zeros[:, 0:P], compare_op=ALU.not_equal,
             fill=1.0, base=0, pattern=[[-1, P]], channel_multiplier=1,
@@ -248,12 +248,10 @@ def tile_list_tabts_silu_kernel(tc, tab_words, tab_scales, w, ts, b, offs, out):
             straight_pass(2, entry, v_codes[:], codes_late[:], scales_moved[:].bitcast(U8))
         for lo, tokens, places in STRAIGHT:
             for h, (bank, column) in enumerate(places):
-                width = P if (lo + tokens == S and h == HALVES - 1) else tokens
-                for at in range(0, tokens, width):
-                    scaled = sbuf(f"scaled{lo + at}_{h}", [P, width], F32)
-                    nc.vector.tensor_tensor(
-                        out=scaled[:], in0=banks[bank][:, column + at : column + at + width],
-                        in1=ts_rows[:, lo + at - FRONT : lo + at - FRONT + width], op=ALU.mult,
-                    )
-                    activate(h, lo + at, width, scaled[:])
-                    store(h, lo + at, lo + at + width)
+                scaled = sbuf(f"scaled{lo}_{h}", [P, tokens], F32)
+                nc.vector.tensor_tensor(
+                    out=scaled[:], in0=banks[bank][:, column : column + tokens],
+                    in1=ts_rows[:, lo - FRONT : lo - FRONT + tokens], op=ALU.mult,
+                )
+                activate(h, lo, tokens, scaled[:])
+                store(h, lo, lo + tokens)

@@ -29,7 +29,7 @@ WORD_BYTES = 4 * T
 TURNED = 2
 FRONT = TURNED * P
 SCALE_CUT = S // 2
-STRAIGHT = [(FRONT, 256, ((2, 0), (3, 0))), (FRONT + 256, 256, ((4, 0), (4, 256))), (S - 256, 256, ((5, 0), (6, 0)))]
+STRAIGHT = [(FRONT, 256, ((2, 0), (2, 256))), (FRONT + 256, 256, ((4, 0), (4, 256))), (S - 256, 256, ((5, 0), (3, 0)))]
 WIDE = 256
 
 
@@ -44,6 +44,7 @@ def tile_list_tabts_silu_kernel(tc, tab_words, tab_scales, w, ts, b, offs, out):
         early_rounded = ctx.enter_context(tc.tile_pool(name="early_rounded", bufs=1))
         first_ts = ctx.enter_context(tc.tile_pool(name="first_ts", bufs=1))
         last_turned = ctx.enter_context(tc.tile_pool(name="last_turned", bufs=1))
+        last_scales = ctx.enter_context(tc.tile_pool(name="last_scales", bufs=1))
         psum = ctx.enter_context(tc.psum_pool(name="psum", bufs=1))
 
         def sbuf(name, shape, dtype):
@@ -131,7 +132,7 @@ def tile_list_tabts_silu_kernel(tc, tab_words, tab_scales, w, ts, b, offs, out):
         ts_banks = banks[6:8]
         ts_cols = placed(first_weights, "ts_cols", [P, blocks], F32, 0)
         ts_first = placed(first_ts, "ts_first", [P, M // 4], F32, 0)
-        ts_front = sbuf("ts_front", [P, TURNED], F32)
+        ts_front = placed(last_scales, "ts_front", [P, P], F32, 0)
         for u in range(blocks):
             place = slice(u % per_bank * P, (u % per_bank + 1) * P)
             nc.tensor.transpose(ts_banks[u // per_bank][:, place], ts_picked[:, u * P : (u + 1) * P], ident[:])
@@ -141,7 +142,7 @@ def tile_list_tabts_silu_kernel(tc, tab_words, tab_scales, w, ts, b, offs, out):
                 in_=bank[:].rearrange("p (u c) -> p u c", c=P)[:, :, TS_ROW],
             )
         nc.scalar.copy(out=ts_first[:, 0:1], in_=ts_banks[0][:, TS_ROW:P])
-        nc.scalar.copy(out=ts_front[:], in_=ts_banks[0][:].rearrange("p (u c) -> p u c", c=P)[:, 0:TURNED, TS_ROW])
+        nc.scalar.copy(out=ts_front[:, 0:TURNED], in_=ts_banks[0][:].rearrange("p (u c) -> p u c", c=P)[:, 0:TURNED, TS_ROW])
         round_w(w_early[1][:], w_raw[1][:])
         for u in range(blocks - TURNED):
             place = slice(u % per_bank * P, (u % per_bank + 1) * P)
@@ -205,16 +206,16 @@ def tile_list_tabts_silu_kernel(tc, tab_words, tab_scales, w, ts, b, offs, out):
         round_w(w_late[:], w_raw[2][:])
         codes_late = placed(early_rounded, "w_codes2", [P, M], U32, 0)
         scales_late = sbuf("w_scales_late", [P, M], U8)
-        quantize_w(w_late[:], codes_late, scales_late[:])
+        quantize_w(w_late[:], codes_late, scales_late[:, 0:M])
         for u in range(TURNED):
             v_block = placed(late, f"v_block{u}", [P, P], U32, raw2 + 4 * P * u)
             gather(v_block, window2, u * P, (u + 1) * P)
-            turned_pass(2, u, v_block[:], codes_late[:], scales_late[:])
-        v_straight = []
-        for lo, tokens, places in STRAIGHT:
-            v_straight.append(placed(late, f"v_straight{lo}", [P, tokens], U32, raw2 + 4 * lo))
-            gather(v_straight[-1], window2, lo, lo + tokens)
-        straight_pass(2, STRAIGHT[0], v_straight[0][:], codes_late[:], scales_late[:])
+            turned_pass(2, u, v_block[:], codes_late[:], scales_late[:, 0:M])
+        v_second = placed(late, "v_second", [P, WIDE], U32, raw2 + 4 * FRONT)
+        gather(v_second, window2, FRONT, S // 2)
+        straight_pass(2, STRAIGHT[0], v_second[:], codes_late[:], scales_late[:, 0:M])
+        v_third = placed(late, "v_third", [P, S // 2 - P], U32, raw2 + 2 * S)
+        gather(v_third, window2, S // 2, S - P)
 
         by_token = [sbuf("by_token0", [P, M], F32), placed(last_turned, "by_token1", [P, S - FRONT + 16], F32, 0)]
         front = [sbuf(f"front{h}", [P, FRONT], F32) for h in range(HALVES)]
@@ -235,18 +236,18 @@ def tile_list_tabts_silu_kernel(tc, tab_words, tab_scales, w, ts, b, offs, out):
                 group = slice(h * P, (h + 1) * P)
                 nc.scalar.activation(out=by_token[u][:, group], in_=banks[u][:, group], func=ACT.Copy, scale=scale)
         scales_moved = placed(first_ts, "scales_moved", [P, M // 4], U32, 0)
-        nc.scalar.copy(out=scales_moved[:], in_=scales_late[:].bitcast(U32))
-        back = (banks[7], banks[0])
-        for h in range(HALVES):
-            for u in range(TURNED):
-                nc.tensor.transpose(back[h][:, u * P : (u + 1) * P], by_token[u][:, h * P : (h + 1) * P], ident[:])
-        for h in range(HALVES):
-            activate(h, 0, FRONT, back[h][:, 0:FRONT])
-            store(h, 0, FRONT)
+        nc.scalar.copy(out=scales_moved[:], in_=scales_late[:, 0:M].bitcast(U32))
+        back = {(0, 0): banks[7], (0, 1): banks[0], (1, 0): banks[6], (1, 1): banks[1]}
+        for u in range(TURNED):
+            for h in range(HALVES):
+                nc.tensor.transpose(back[u, h][:, 0:P], by_token[u][:, h * P : (h + 1) * P], ident[:])
+        for u in range(TURNED):
+            for h in range(HALVES):
+                activate(h, u * P, P, back[u, h][:, 0:P])
+                store(h, u * P, (u + 1) * P)
 
-        for entry, v_codes in zip(STRAIGHT[1:], v_straight[1:]):
-            straight_pass(2, entry, v_codes[:], codes_late[:], scales_moved[:].bitcast(U8))
-        for lo, tokens, places in STRAIGHT:
+        def finish(entry):
+            lo, tokens, places = entry
             for h, (bank, column) in enumerate(places):
                 scaled = sbuf(f"scaled{lo}_{h}", [P, tokens], F32)
                 nc.vector.tensor_tensor(
@@ -255,3 +256,20 @@ def tile_list_tabts_silu_kernel(tc, tab_words, tab_scales, w, ts, b, offs, out):
                 )
                 activate(h, lo, tokens, scaled[:])
                 store(h, lo, lo + tokens)
+
+        finish(STRAIGHT[0])
+        moved = scales_moved[:].bitcast(U8)
+        straight_pass(2, STRAIGHT[1], v_third[:, 0:WIDE], codes_late[:], moved)
+        v_last = placed(last_scales, "v_last", [P, P], U32, 0)
+        gather(v_last, window2, S - P, S)
+        lo, tokens, places = STRAIGHT[2]
+        for at, v_codes in ((0, v_third[:, WIDE : WIDE + P]), (P, v_last[:])):
+            for h, (bank, column) in enumerate(places):
+                nc.tensor.matmul_mx(
+                    out=banks[bank][:, column + at : column + at + P],
+                    lhsT=codes_late[:, h * P : (h + 1) * P].bitcast(FP8X4), lhsT_scale=moved[:, h * P : (h + 1) * P],
+                    rhs=v_codes.bitcast(FP8X4), rhs_scale=part_of(scale_parts, SCALE_CUT, lo + at, P)[4 * (PASSES - 1) : P, :],
+                    start=False, stop=(at == P),
+                )
+        finish(STRAIGHT[1])
+        finish(STRAIGHT[2])

@@ -29,7 +29,7 @@ WORD_BYTES = 4 * T
 TURNED = 2
 FRONT = TURNED * P
 SCALE_CUT = S // 2
-STRAIGHT = [(FRONT, 256, ((2, 0), (2, 256))), (FRONT + 256, 256, ((4, 0), (4, 256))), (S - 256, 256, ((5, 0), (3, 0)))]
+STRAIGHT = [(FRONT, 256, ((2, 0), (6, 0))), (FRONT + 256, 256, ((4, 0), (4, 256))), (S - 256, 256, ((5, 0), (3, 0)))]
 WIDE = 256
 
 
@@ -129,7 +129,7 @@ def tile_list_tabts_silu_kernel(tc, tab_words, tab_scales, w, ts, b, offs, out):
 
         blocks = S // P
         per_bank = BANK // P
-        ts_banks = banks[6:8]
+        ts_banks = [banks[7], banks[3]]
         ts_cols = placed(first_weights, "ts_cols", [P, blocks], F32, 0)
         ts_first = placed(first_ts, "ts_first", [P, M // 4], F32, 0)
         ts_front = placed(last_scales, "ts_front", [P, P], F32, 0)
@@ -213,7 +213,6 @@ def tile_list_tabts_silu_kernel(tc, tab_words, tab_scales, w, ts, b, offs, out):
             turned_pass(2, u, v_block[:], codes_late[:], scales_late[:, 0:M])
         v_second = placed(late, "v_second", [P, WIDE], U32, raw2 + 4 * FRONT)
         gather(v_second, window2, FRONT, S // 2)
-        straight_pass(2, STRAIGHT[0], v_second[:], codes_late[:], scales_late[:, 0:M])
         v_third = placed(late, "v_third", [P, S // 2 - P], U32, raw2 + 2 * S)
         gather(v_third, window2, S // 2, S - P)
 
@@ -230,21 +229,24 @@ def tile_list_tabts_silu_kernel(tc, tab_words, tab_scales, w, ts, b, offs, out):
         def store(h, lo, hi):
             nc.sync.dma_start(out=out[h * P : (h + 1) * P, lo:hi], in_=result(h, lo, hi))
 
-        for u in range(TURNED):
-            scale = ts_first[:, 0:1] if u == 0 else ts_front[:, u : u + 1]
-            for h in range(HALVES):
-                group = slice(h * P, (h + 1) * P)
-                nc.scalar.activation(out=by_token[u][:, group], in_=banks[u][:, group], func=ACT.Copy, scale=scale)
+        def scale_out(u, h, columns):
+            group = slice(h * P, (h + 1) * P)
+            nc.scalar.activation(out=by_token[u][:, group], in_=banks[u][:, group], func=ACT.Copy, scale=columns[:, u : u + 1])
+
+        pieces = [(u, h) for u in range(TURNED) for h in range(HALVES)]
+        for u, h in pieces[:-1]:
+            scale_out(u, h, ts_first if u == 0 else ts_front)
         scales_moved = placed(first_ts, "scales_moved", [P, M // 4], U32, 0)
         nc.scalar.copy(out=scales_moved[:], in_=scales_late[:, 0:M].bitcast(U32))
-        back = {(0, 0): banks[7], (0, 1): banks[0], (1, 0): banks[6], (1, 1): banks[1]}
-        for u in range(TURNED):
-            for h in range(HALVES):
-                nc.tensor.transpose(back[u, h][:, 0:P], by_token[u][:, h * P : (h + 1) * P], ident[:])
-        for u in range(TURNED):
-            for h in range(HALVES):
-                activate(h, u * P, P, back[u, h][:, 0:P])
-                store(h, u * P, (u + 1) * P)
+        scale_out(*pieces[-1], ts_front)
+        back = {(0, 0): banks[7][:, 0:P], (0, 1): banks[7][:, P : 2 * P], (1, 0): banks[0][:, 0:P], (1, 1): banks[1][:, 0:P]}
+        for u, h in pieces:
+            nc.tensor.transpose(back[u, h], by_token[u][:, h * P : (h + 1) * P], ident[:])
+        moved = scales_moved[:].bitcast(U8)
+        straight_pass(2, STRAIGHT[0], v_second[:], codes_late[:], moved)
+        for u, h in pieces:
+            activate(h, u * P, P, back[u, h])
+            store(h, u * P, (u + 1) * P)
 
         def finish(entry):
             lo, tokens, places = entry
@@ -258,7 +260,6 @@ def tile_list_tabts_silu_kernel(tc, tab_words, tab_scales, w, ts, b, offs, out):
                 store(h, lo, lo + tokens)
 
         finish(STRAIGHT[0])
-        moved = scales_moved[:].bitcast(U8)
         straight_pass(2, STRAIGHT[1], v_third[:, 0:WIDE], codes_late[:], moved)
         v_last = placed(last_scales, "v_last", [P, P], U32, 0)
         gather(v_last, window2, S - P, S)

from contextlib import ExitStack

import concourse.mybir as mybir

K, M, T, S = 1536, 256, 2048, 1024
FLOPS = 2 * K * M * S
BYTES = K * T + (K // 32) * T + 4 * K * M + 4 * T + 4 * M + 2 * 128 * (S // 16) + 4 * M * S

F32 = mybir.dt.float32
BF16 = mybir.dt.bfloat16
I32 = mybir.dt.int32
U32 = mybir.dt.uint32
U16 = mybir.dt.uint16
U8 = mybir.dt.uint8
FP8X4 = mybir.dt.float8_e4m3fn_x4
ACT = mybir.ActivationFunctionType
ALU = mybir.AluOpType

P = 128
PACK = 4
K_PASS = P * PACK
PASSES = K // K_PASS
QUADRANTS = (0, 1, 2, 3)
BANK = 512
HALVES = M // P
TS_ROW = P - 1
RAW_BYTES = PACK * M * 4
WORD_BYTES = 4 * T
TURNED = 2
FRONT = TURNED * P
SCALE_CUT = S // 2
STRAIGHT = [(FRONT, 256, ((2, 0), (6, 0))), (FRONT + 256, 256, ((4, 0), (4, 256))), (S - 256, 256, ((5, 0), (3, 0)))]
WIDE = 256


def tile_list_tabts_silu_kernel(tc, tab_words, tab_scales, w, ts, b, offs, out):
    nc = tc.nc
    with ExitStack() as ctx:
        keep = ctx.enter_context(tc.tile_pool(name="keep", bufs=1))
        late = ctx.enter_context(tc.tile_pool(name="late", bufs=1))
        first_words = ctx.enter_context(tc.tile_pool(name="first_words", bufs=1))
        first_weights = ctx.enter_context(tc.tile_pool(name="first_weights", bufs=1))
        picked_ts = ctx.enter_context(tc.tile_pool(name="picked_ts", bufs=1))
        early_rounded = ctx.enter_context(tc.tile_pool(name="early_rounded", bufs=1))
        first_ts = ctx.enter_context(tc.tile_pool(name="first_ts", bufs=1))
        last_turned = ctx.enter_context(tc.tile_pool(name="last_turned", bufs=1))
        last_scales = ctx.enter_context(tc.tile_pool(name="last_scales", bufs=1))
        psum = ctx.enter_context(tc.psum_pool(name="psum", bufs=1))

        def sbuf(name, shape, dtype):
            return keep.tile(shape, dtype, name=name, align_bytes=64)

        def placed(pool, name, shape, dtype, offset):
            return pool.tile(shape, dtype, name=name, offset=offset, align_bytes=64)

        offsets = keep.tile([P, S // 16], U16, name="offsets")
        ts_window = sbuf("ts_window", [P, T], F32)
        scale_window = sbuf("scale_window", [P, T // 4], I32)
        ts_picked = placed(picked_ts, "ts_picked", [P, S], F32, 0)
        ident = sbuf("ident", [P, P], F32)
        banks = [psum.tile([P, BANK], F32, name=f"bank{i}") for i in range(8)]

        def load_words(a, window):
            nc.sync.dma_start(out=window[:], in_=tab_words[a].rearrange("p t i -> p (t i)").bitcast(I32))

        def load_w(a, raw):
            rows = w[K_PASS * a : K_PASS * (a + 1), :]
            nc.sync.dma_start(out=raw[:], in_=rows.rearrange("(p i) n -> p i n", i=PACK))

        nc.sync.dma_start(offsets[:], offs)
        nc.scalar.dma_start(out=ts_window[TS_ROW:P, :], in_=ts[0:1, :])
        nc.vector.memset(scale_window[:], 0)

        zeros = placed(late, "zeros", [P, (2 * WORD_BYTES + 3 * RAW_BYTES) // 4 + 16], F32, 0)
        nc.vector.memset(zeros[:, 0:P], 0.0)
        nc.vector.memset(ts_window[0:TS_ROW, :], 0.0)
        nc.gpsimd.affine_select(
            out=ident[:], in_=zeros[:, 0:P], compare_op=ALU.not_equal,
            fill=1.0, base=0, pattern=[[-1, P]], channel_multiplier=1,
        )

        raw1 = 2 * WORD_BYTES + RAW_BYTES // 2
        raw2 = 2 * WORD_BYTES + 2 * RAW_BYTES
        windows = [
            placed(first_words, "word_window0", [P, T], I32, 0),
            placed(late, "word_window1", [P, T], I32, 0),
            placed(late, "word_window2", [P, T], I32, WORD_BYTES),
        ]
        w_raw = [
            placed(first_weights, "w_raw0", [P, PACK, M], F32, 0),
            placed(late, "w_raw1", [P, PACK, M], F32, raw1),
            placed(late, "w_raw2", [P, PACK, M], F32, raw2),
        ]
        bias = placed(late, "bias", [P, HALVES], F32, raw2 + RAW_BYTES)

        load_words(0, windows[0])
        load_w(0, w_raw[0])
        for q in QUADRANTS:
            nc.sync.dma_start(
                out=scale_window[32 * q : 32 * q + 4 * PASSES, :],
                in_=tab_scales[:, 4 * q : 4 * q + 4, :].bitcast(I32),
            )
        load_w(1, w_raw[1])
        load_words(1, windows[1])
        load_w(2, w_raw[2])
        load_words(2, windows[2])
        with nc.allow_non_contiguous_dma(reason="one bias value a partition"):
            nc.sync.dma_start(out=bias[:], in_=b.rearrange("(h p) -> p h", p=P))

        def gather(picked, window, lo=0, hi=S):
            nc.vector.tensor_copy(out=picked[:], in_=window.indirect(offsets[:, lo // 16 : hi // 16]))

        def round_w(rounded, raw):
            nc.scalar.copy(
                out=rounded.rearrange("p (c j) i -> p c i j", j=4),
                in_=raw.rearrange("p i (c j) -> p c i j", j=4),
            )

        def quantize_w(rounded, codes, scales):
            nc.vector.quantize_mx(
                out=codes[:].bitcast(FP8X4), scales=scales, in_=rounded.rearrange("p n i -> p (n i)")
            )

        gather(ts_picked, ts_window[:])
        w_early = [sbuf("w_early0", [P, M, PACK], BF16), placed(early_rounded, "w_early1", [P, M, PACK], BF16, 0)]
        warm = sbuf("warm", [P, 1], F32)
        nc.scalar.activation(out=warm[:], in_=w_raw[0][:, 0, 0:1], func=ACT.Silu)
        round_w(w_early[0][:], w_raw[0][:])

        blocks = S // P
        per_bank = BANK // P
        ts_banks = [banks[7], banks[3]]
        ts_cols = placed(first_weights, "ts_cols", [P, blocks], F32, 0)
        ts_first = placed(first_ts, "ts_first", [P, M // 4], F32, 0)
        ts_front = placed(last_scales, "ts_front", [P, P], F32, 0)
        for u in range(blocks):
            place = slice(u % per_bank * P, (u % per_bank + 1) * P)
            nc.tensor.transpose(ts_banks[u // per_bank][:, place], ts_picked[:, u * P : (u + 1) * P], ident[:])
        for i, bank in enumerate(ts_banks):
            nc.scalar.copy(
                out=ts_cols[:, per_bank * i : per_bank * (i + 1)],
                in_=bank[:].rearrange("p (u c) -> p u c", c=P)[:, :, TS_ROW],
            )
        nc.scalar.copy(out=ts_first[:, 0:1], in_=ts_banks[0][:, TS_ROW:P])
        nc.scalar.copy(out=ts_front[:, 0:TURNED], in_=ts_banks[0][:].rearrange("p (u c) -> p u c", c=P)[:, 0:TURNED, TS_ROW])
        round_w(w_early[1][:], w_raw[1][:])
        for u in range(blocks - TURNED):
            place = slice(u % per_bank * P, (u % per_bank + 1) * P)
            column = ts_cols[:, TURNED + u : TURNED + u + 1]
            nc.tensor.transpose(ts_banks[u // per_bank][:, place], column.to_broadcast([P, P]), ident[:])
        ts_rows = placed(late, "ts_rows", [P, S - FRONT], F32, 2 * WORD_BYTES)
        for i, bank in enumerate(ts_banks):
            width = min(BANK, S - FRONT - i * BANK)
            nc.scalar.copy(out=ts_rows[:, i * BANK : i * BANK + width], in_=bank[:, 0:width])

        def turned_pass(a, u, v_codes, w_codes, w_scales):
            nc.tensor.matmul_mx(
                out=banks[u][:, 0:M],
                lhsT=v_codes.bitcast(FP8X4), lhsT_scale=part_of(scale_parts, SCALE_CUT, u * P, P)[4 * a : P, :],
                rhs=w_codes.bitcast(FP8X4), rhs_scale=w_scales,
                start=(a == 0), stop=(a == PASSES - 1),
            )

        def straight_pass(a, entry, v_codes, w_codes, w_scales):
            lo, tokens, places = entry
            shared = places[0][0] == places[1][0]
            for h, (bank, column) in enumerate(places):
                for at in range(0, tokens, WIDE):
                    end = min(at + WIDE, tokens)
                    nc.tensor.matmul_mx(
                        out=banks[bank][:, column + at : column + end],
                        lhsT=w_codes[:, h * P : (h + 1) * P].bitcast(FP8X4), lhsT_scale=w_scales[:, h * P : (h + 1) * P],
                        rhs=v_codes[:, at:end].bitcast(FP8X4), rhs_scale=part_of(scale_parts, SCALE_CUT, lo + at, end - at)[4 * a : P, :],
                        start=(a == 0 and column + at == 0),
                        stop=(a == PASSES - 1 and end == tokens and (h == HALVES - 1 or not shared)),
                    )

        def whole_pass(a, codes_of, w_codes, w_scales):
            for u in range(TURNED):
                turned_pass(a, u, codes_of(u * P, P), w_codes, w_scales)
            for entry in STRAIGHT:
                straight_pass(a, entry, codes_of(entry[0], entry[1]), w_codes, w_scales)

        def part_of(parts, cut, lo, n):
            return parts[0][:, lo : lo + n] if lo < cut else parts[1][:, lo - cut : lo - cut + n]

        v_codes0 = sbuf("v_codes0", [P, S], U32)
        gather(v_codes0, windows[0][:].bitcast(U32))
        scale_parts = [placed(picked_ts, "v_scales0", [P, SCALE_CUT], U8, 0), placed(first_weights, "v_scales1", [P, S - SCALE_CUT], U8, 1024)]
        gather(scale_parts[0], scale_window[:].bitcast(U8), 0, SCALE_CUT)
        w_codes = [sbuf(f"w_codes{a}", [P, M], U32) for a in range(2)]
        w_scales = [sbuf(f"w_scales{a}", [P, M], U8) for a in range(2)]
        quantize_w(w_early[0][:], w_codes[0], w_scales[0][:])
        gather(scale_parts[1], scale_window[:].bitcast(U8), SCALE_CUT, S)
        whole_pass(0, lambda lo, n: v_codes0[:, lo : lo + n], w_codes[0][:], w_scales[0][:])

        quantize_w(w_early[1][:], w_codes[1], w_scales[1][:])
        at = 2 * WORD_BYTES + 4 * (S - FRONT)
        parts = [placed(late, "v_codes1a", [P, S // 2], U32, at), placed(late, "v_codes1b", [P, S // 2], U32, at + 2 * S)]
        gather(parts[0], windows[1][:].bitcast(U32), 0, S // 2)
        gather(parts[1], windows[1][:].bitcast(U32), S // 2, S)
        whole_pass(1, lambda lo, n: part_of(parts, S // 2, lo, n), w_codes[1][:], w_scales[1][:])

        window2 = windows[2][:].bitcast(U32)
        w_late = sbuf("w_late", [P, M, PACK], BF16)
        round_w(w_late[:], w_raw[2][:])
        codes_late = placed(early_rounded, "w_codes2", [P, M], U32, 0)
        scales_late = sbuf("w_scales_late", [P, M], U8)
        quantize_w(w_late[:], codes_late, scales_late[:, 0:M])
        for u in range(TURNED):
            v_block = placed(late, f"v_block{u}", [P, P], U32, raw2 + 4 * P * u)
            gather(v_block, window2, u * P, (u + 1) * P)
            turned_pass(2, u, v_block[:], codes_late[:], scales_late[:, 0:M])
        v_second = placed(late, "v_second", [P, WIDE], U32, raw2 + 4 * FRONT)
        gather(v_second, window2, FRONT, S // 2)
        v_third = placed(late, "v_third", [P, S // 2 - P], U32, raw2 + 2 * S)
        gather(v_third, window2, S // 2, S - P)

        by_token = [sbuf("by_token0", [P, M], F32), placed(last_turned, "by_token1", [P, S - FRONT + 16], F32, 0)]
        front = [sbuf(f"front{h}", [P, FRONT], F32) for h in range(HALVES)]
        rest = [placed(last_turned, f"rest{h}", [P, S - FRONT], F32, 4 * (S - FRONT) * h) for h in range(HALVES)]

        def result(h, lo, hi):
            return front[h][:, lo:hi] if lo < FRONT else rest[h][:, lo - FRONT : hi - FRONT]

        def activate(h, lo, tokens, scaled):
            nc.scalar.activation(out=result(h, lo, lo + tokens), in_=scaled, func=ACT.Silu, bias=bias[:, h : h + 1])

        def store(h, lo, hi):
            nc.sync.dma_start(out=out[h * P : (h + 1) * P, lo:hi], in_=result(h, lo, hi))

        def scale_out(u, h, columns):
            group = slice(h * P, (h + 1) * P)
            nc.scalar.activation(out=by_token[u][:, group], in_=banks[u][:, group], func=ACT.Copy, scale=columns[:, u : u + 1])

        pieces = [(u, h) for u in range(TURNED) for h in range(HALVES)]
        for u, h in pieces[:-1]:
            scale_out(u, h, ts_first if u == 0 else ts_front)
        scales_moved = placed(first_ts, "scales_moved", [P, M // 4], U32, 0)
        nc.scalar.copy(out=scales_moved[:], in_=scales_late[:, 0:M].bitcast(U32))
        scale_out(*pieces[-1], ts_front)
        back = {(0, 0): banks[7][:, 0:P], (0, 1): banks[7][:, P : 2 * P], (1, 0): banks[0][:, 0:P], (1, 1): banks[1][:, 0:P]}
        for u, h in pieces:
            nc.tensor.transpose(back[u, h], by_token[u][:, h * P : (h + 1) * P], ident[:])
        moved = scales_moved[:].bitcast(U8)
        straight_pass(2, STRAIGHT[0], v_second[:], codes_late[:], moved)
        for u, h in pieces:
            activate(h, u * P, P, back[u, h])
            store(h, u * P, (u + 1) * P)

        def finish(entry):
            lo, tokens, places = entry
            for h, (bank, column) in enumerate(places):
                scaled = sbuf(f"scaled{lo}_{h}", [P, tokens], F32)
                nc.vector.tensor_tensor(
                    out=scaled[:], in0=banks[bank][:, column : column + tokens],
                    in1=ts_rows[:, lo - FRONT : lo - FRONT + tokens], op=ALU.mult,
                )
                activate(h, lo, tokens, scaled[:])
                store(h, lo, lo + tokens)

        finish(STRAIGHT[0])
        straight_pass(2, STRAIGHT[1], v_third[:, 0:WIDE], codes_late[:], moved)
        v_last = placed(last_scales, "v_last", [P, P], U32, 0)
        gather(v_last, window2, S - P, S)
        lo, tokens, places = STRAIGHT[2]
        for at, v_codes in ((0, v_third[:, WIDE : WIDE + P]), (P, v_last[:])):
            for h, (bank, column) in enumerate(places):
                nc.tensor.matmul_mx(
                    out=banks[bank][:, column + at : column + at + P],
                    lhsT=codes_late[:, h * P : (h + 1) * P].bitcast(FP8X4), lhsT_scale=moved[:, h * P : (h + 1) * P],
                    rhs=v_codes.bitcast(FP8X4), rhs_scale=part_of(scale_parts, SCALE_CUT, lo + at, P)[4 * (PASSES - 1) : P, :],
                    start=False, stop=(at == P),
                )
        finish(STRAIGHT[1])
        finish(STRAIGHT[2])
